import numpy as np, ml_dtypes
CORES = [5,29,101,125,133,157,229,253]
N = 8
import mx_ref
BF = ml_dtypes.bfloat16
def gentries(a):
    return np.ascontiguousarray(a.reshape(8, 16, -1).transpose(0, 2, 1)).reshape(8, -1)
def gtable(e):
    e = np.asarray(e); return np.ascontiguousarray(e.reshape(8, -1, 16).transpose(0, 2, 1)).reshape(128, -1).astype(np.int32)
def gcols(t, e):
    v = np.concatenate([t.reshape(8, 16, -1, 4), np.zeros((8, 16, 1, 4), BF)], axis=2)
    return np.ascontiguousarray(np.stack([v[g][:, e[g]] for g in range(8)])).reshape(128, -1)
def tile(rs):
    return np.stack(rs, axis=2).reshape(128, -1).astype(BF)
def cut(t, i, w=512):
    return t[:, w * i:w * i + w]
def pick(q, e):
    c = np.concatenate([q[0].reshape(128, -1, 4), np.zeros((128, 1, 4), np.uint8)], axis=1); s = np.concatenate([q[1], np.ones((16, 1), np.uint8)], axis=1)
    return (np.ascontiguousarray(c[:, e].reshape(128, -1)), np.ascontiguousarray(s[:, e]))
def join(*qs):
    return (np.concatenate([q[0] for q in qs], axis=1), np.concatenate([q[1] for q in qs], axis=1))
def put(q, e, v):
    c, s = q[0].reshape(128, -1, 4).copy(), q[1].copy(); c[:, e] = v[0].reshape(128, -1, 4); s[:, e] = v[1]
    return (c.reshape(128, -1), s)
def pk(c, s):
    return (np.ascontiguousarray(c), mx_ref.live(s))
def emit(q):
    return q[0], q[1]
def packed(v, rng):
    q = [mx_ref.quantize(np.ascontiguousarray(v[r])) for r in range(N)]
    return np.stack([a for a, b in q]), np.stack([mx_ref.plane(b, rng) for a, b in q])
def values_of_codes():
    e, c = np.zeros((128, 128, 4), np.float32), np.zeros((128, 2, 4), np.uint8)
    e[np.arange(128), np.arange(128), 0] = 1
    c[:127, :, 0] = np.arange(256).reshape(2, 128).T[:127]
    return mx_ref.matmul(mx_ref.quantize(e.reshape(128, 512).astype(BF)), (c.reshape(128, 8), np.full((16, 2), 127, np.uint8))).T.reshape(-1).astype(np.float64)
CODE_VALUE, SCALE_VALUE = values_of_codes(), 2.0 ** (np.arange(256) - 127.0)
def decode(q):
    return (CODE_VALUE[q[0]].reshape(16, 8, -1, 4) * SCALE_VALUE[q[1]][:, None, :, None] + 0.0).reshape(128, -1).astype(np.float32)
def f(rng, *shape):
    return mx_ref.flush((rng.standard_normal(shape, dtype=np.float32) * np.exp2(rng.integers(-2, 3, shape[:-1] + (1,)))).astype(BF))
def wide(rng, *shape, cols=0):
    v = rng.standard_normal(shape, dtype=np.float32) * np.exp2(rng.integers(-12, 13, shape)).astype(np.float32)
    if cols: v *= np.repeat(np.exp2(rng.integers(-cols, cols + 1, shape[:-2] + (1, shape[-1] // 4))) * (rng.random(shape[:-2] + (1, shape[-1] // 4)) > 0.0625), 4, axis=-1).astype(np.float32)
    return mx_ref.flush(v.astype(BF))
C, K, R = 448, 224, 3
def living(z):
    return np.sort(np.argsort(-(z[::16] + np.float32(0.0)), axis=1, kind="stable")[:, :K], axis=1)
def ancestors(p, e, alive):
    to = np.where(alive, np.arange(C), p)
    for k in range(9): to = np.take_along_axis(to, to, axis=1)
    a = np.take_along_axis(to, np.take_along_axis(p, e, axis=1), axis=1)
    return np.where(np.take_along_axis(alive, a, axis=1), a, e)
def cleared(v):
    v = v.astype(np.float32)
    v[np.abs(v) < np.float32(2.0 ** -16)] = 0
    return v.astype(BF)
def pointers(rng):
    w = 2 ** rng.integers(1, 10, (N, 8, 1))
    back = rng.integers(1, w + 1, (N, 8, C))
    back[rng.random((N, 8, C)) < 0.03125] = 0
    e = np.maximum(np.arange(C) - back, 0)
    return np.stack([gtable(e[r]) for r in range(N)])
def numbers_of(rng):
    return {"x": cleared(f(rng, N, 128, 4 * C)), "ptr": pointers(rng), "u": np.array(f(rng, N, 128, 512))}
def weights(rng, w):
    c, p = packed(w, rng)
    return {"wc": c, "ws": p}
def still(rng, gs=(), hs=()):
    w = np.zeros((N, 128, 4, 128, 4), np.float32)
    i = np.arange(128)
    for b in range(4): w[:, i, b, i, b] = 32
    for g in gs:
        w[:, 16 * g, 0, 16 * g, 0] = 128
        w[:, 16 * g + 2, 0, 16 * g + 2, 0] = 0
    for g in hs: w[:, 16 * g + 4, 0, 16 * g + 4, 0] = 36
    return weights(rng, w.reshape(N, 128, 2048).astype(BF))
def signs(rng):
    return np.stack([rng.permutation(8) % 2 * 2.0 - 1.0 for r in range(N)]).astype(np.float32)
def setup_inputs(rng):
    return {**numbers_of(rng), **weights(rng, f(rng, N, 128, 2048))}
def setup_inputs_ties(rng):
    d = numbers_of(rng)
    n = rng.permutation(N)
    x = d["x"].reshape(N, 8, 16, C, 4)
    for r in range(N):
        for g in range(8):
            k = np.zeros(C, int) if r == n[0] else rng.permutation(C) % 3
            a = x[r, g, :8, :3].copy()
            a[:, 2] = 0
            x[r, g, :8] = a[:, k]
    x[n[1]] = 0
    u = d["u"].reshape(N, 8, 16, 8, 16, 4)
    b = np.zeros((N, 8, 16, 8, 4), BF)
    for g in range(8): b[:, g, :8, g] = u[:, g, :8, g, 0]
    u[:, :, :, :, 0] = b
    w = f(rng, N, 128, 2048).astype(np.float32).reshape(N, 8, 16, 4, 8, 16, 4)
    w[:, :, 8:, :, :, :8] = 0
    for g in range(8):
        for h in range(8):
            if g != h: w[:, g, :, :, h, :8] = 0
    w[:, :, :, :, :, :8] *= 4
    return {"x": x.reshape(N, 128, 4 * C), "ptr": d["ptr"], "u": u.reshape(N, 128, 512), **weights(rng, w.reshape(N, 128, 2048).astype(BF))}
def setup_inputs_near(rng):
    d = numbers_of(rng)
    x = d["x"].astype(np.float32).reshape(N, 8, 16, C, 4)
    s = (np.arange(C) // 2 + rng.integers(0, C // 4, (N, 8, 1))) % (C // 2)
    g = ((s[..., None] >> np.arange(8)) & 1) * np.exp2(np.arange(8) - 23.0)
    v = np.stack([rng.permutation(8) for r in range(N)])
    k = (v % 2 * 2.0 - 1.0).astype(np.float32)
    size = np.where(v < 4, 1.0, 2.0 ** -30).astype(np.float32)
    x[:, :, 0] = 0
    x[:, :, 0, :, 0] = 1
    for r in rng.permutation(N)[:N // 2]:
        for h in range(8):
            x[r, h, 0, rng.choice(np.flatnonzero(s[r, h] == C // 2 - 1)), 0] = k[r, h] * 2.0 ** 30
            x[r, h, 0, rng.choice(np.flatnonzero(s[r, h] == 0)), 0] = k[r, h] * -2.0 ** 30
    x[:, :, 8] = g[..., :4]
    x[:, :, 9] = g[..., 4:]
    x[:, :, 10:] = rng.integers(4, 8, (N, 8, 6, C, 4)) * rng.choice([-1.0, 1.0], (N, 8, 6, C, 4)) * 2.0 ** -20
    u = d["u"].reshape(N, 128, 128, 4)
    u[:, :, ::16] = 0
    for h in range(0, 128, 16):
        c = size[:, h // 16]
        u[:, h, h, 0] = (k[:, h // 16] * c).astype(BF)
        u[:, h + 8:h + 10, h] = c[:, None, None].astype(BF)
    return {"x": x.reshape(N, 128, 4 * C).astype(BF), "ptr": d["ptr"], "u": u.reshape(N, 128, 512), **still(rng)}
def setup_inputs_huge(rng):
    d = numbers_of(rng)
    x = 2.0 ** 30 * (0.6 + 0.4 * rng.random((N, 128, C, 4)))
    c = np.ones((N, C))
    for r in rng.permutation(N)[:N // 4]: c[r, rng.permutation(C) % 3 == 0] = -1
    x *= c[:, None, :, None]
    u = d["u"].reshape(N, 128, 128, 4)
    a = 2.0 ** 30 * (1 - 0.25 * rng.random((N, 128, 8, 4))) * signs(rng)[:, None, :, None]
    u[:, :, ::16] = a.astype(np.float32).astype(BF)
    return {"x": x.astype(np.float32).reshape(N, 128, 4 * C).astype(BF), "ptr": d["ptr"], "u": u.reshape(N, 128, 512), **still(rng)}
def setup_inputs_deep(rng):
    d = numbers_of(rng)
    x = d["x"].reshape(N, 8, 16, C, 4)
    u = d["u"].reshape(N, 8, 16, 8, 16, 4)
    u[:, :, :, :, 0] = 0
    kind = rng.permutation([0, 0, 1, 1, 2, 3, 3, 4])
    e = np.stack([gentries(d["ptr"][r]) for r in range(N)])
    e[:, kind != 2] = np.maximum(np.arange(C) - 1, 0)
    e[:, kind == 4] = np.arange(C)
    step = SCALE_VALUE[mx_ref.quantize(np.full((128, 16), 28.0, np.float32).astype(BF))[1][0, 0]] * 2.0 ** -9
    small = (np.where(np.arange(C) < K + K // 2, 3, 5) * step).astype(np.float32).astype(BF)
    for g in range(8):
        alive = np.arange(C) > K if kind[g] == 0 else np.arange(C) >= K
        a = np.where(alive, 4.0, -4.0).astype(np.float32)
        if kind[g] == 0: a[0] = 8
        if kind[g] == 4: a[K:K + K // 2] = 12
        o = 8 if kind[g] == 4 else 0
        for r in range(N):
            b = np.where(alive, (16.0, 8.0, 0.0, 8.0 - 8.0 * (r % 2), 8.0)[kind[g]], 0.0).astype(np.float32)
            x[r, g, o + r % 2, :, 0] = a.astype(BF)
            x[r, g, o + 1 - r % 2, :, 0] = b.astype(BF)
            u[r, g, o + r % 2, g, 0, 0] = 1
            if kind[g] == 3:
                x[r, g, 2, :, 0] = 0
                if r % 2 == 0:
                    x[r, g, 0, K, 0] = 3
                    x[r, g, 2, K, 0] = 64
                    u[r, g, 2, g, 0, 0] = 1
            if kind[g] == 4:
                x[r, g, :8] = 0
                x[r, g, 3, :, 0] = small
                x[r, g, 4, :, 0] = 28
                u[r, g, 3, g, 0, 0] = 1
    return {"x": x.reshape(N, 128, 4 * C), "ptr": np.stack([gtable(e[r]) for r in range(N)]), "u": u.reshape(N, 128, 512), **still(rng, np.flatnonzero(kind == 3), np.flatnonzero(kind == 4))}
def setup_inputs_spread(rng):
    d = setup_inputs(rng)
    d["x"] = cleared(wide(rng, N, 128, 4 * C, cols=6))
    return d
def check_inputs(d):
    b = []
    for k in ("x", "u"):
        a = np.abs(d[k].astype(np.float32))
        if not (np.isfinite(a).all() and ((a == 0) | (a >= 2.0 ** -30) & (a <= 2.0 ** 30)).all()): b.append("a value of " + k)
    for p in d["ptr"]:
        e = gentries(p)
        if ((e < 0) | (e > np.arange(C))).any():
            b.append("an entry of ptr")
            break
    return b
def reference(x, ptr, u, wc, ws):
    qu = [mx_ref.quantize(u[r]) for r in range(N)]
    lay = [pk(wc[r], ws[r]) for r in range(N)]
    now = [x[r] for r in range(N)]
    point = [gentries(ptr[r]) for r in range(N)]
    for t in range(R):
        blend, sent = [], []
        for r in range(N):
            e = living(mx_ref.matmul(qu[r], mx_ref.quantize(now[r])))
            number = np.full((8, C), -1)
            np.put_along_axis(number, e, np.arange(K)[None, :], axis=1)
            a = ancestors(point[r], e, number >= 0)
            s = ((gcols(now[r], e).astype(np.float32) + gcols(now[r], a).astype(np.float32)) * np.float32(0.5)).astype(BF)
            q = mx_ref.quantize(s)
            h = tile([np.maximum(mx_ref.matmul(pick(lay[r], np.arange(128 * b, 128 * b + 128)), q), np.float32(0.0)) * np.float32(0.03125) for b in range(4)])
            blend.append(s)
            sent.append(mx_ref.quantize(h))
            point[r] = np.concatenate([np.take_along_axis(number, a, axis=1), np.tile(np.arange(K), (8, 1))], axis=1)
        came = decode(join(*sent)).astype(BF)
        for r in range(N): now[r] = np.concatenate([blend[r], cut(came, (r - 1) % N, 4 * K)], axis=1)
    y, pl = np.zeros((N, 128, C), np.float32), np.zeros((N, 8, C), np.float32)
    oc, osc = np.zeros((N, 128, 4 * C), np.uint8), np.zeros((N, 16, C), np.uint8)
    for r in range(N):
        q = mx_ref.quantize(now[r])
        y[r] = mx_ref.matmul(qu[r], q)
        pl[r] = point[r]
        oc[r], osc[r] = emit(q)
    return {"y": y, "pl": pl, "oc": oc, "osc": osc}

@@ -1,0 +1,466 @@
+from concourse.bass import DstId, RemoteDMATransfer
+from concourse.mybir import dt, AluOpType, ActivationFunctionType
+
+C, K, R, NK = 448, 224, 3, 14
+FW = K + 16
+RW = C + 16
+BIG = 1e29
+LIFT = 1024.0
+SHARE = {C: [2, 3, 3, 3, 3], K: [3, 3, 3, 3, 2]}
+SPLIT = {C: [14, 14, 20, 14], K: [14, 14, 14, 8]}
+NH = 8
+CODE = "float8_e4m3fn_x4"
+
+BUFFERS = {
+    "bfloat16": {"xt": 4 * C, "xh": 4 * C, "ut": 512, "ht": 4 * K, "vh": 4 * K, "et": 520, "one": 520, "iom": RW,
+                 "cap": C, "keep": K, "fa": NK * K, "fb": NK * K, "junk": NK * FW, "eq": K, "es": K, "krow": K, "f": C,
+                 "cb": K, "cum": C, "ra": RW, "rb": RW, "rc": RW, "pr": K, "exb": C, "xr": K},
+    "float16": {"ms": C},
+    "float32": {"iot": RW, "w16": 80, "off": 8, "qf": 8, "mk": K, "rst": K, "il": 32, "nl": 16, "c2": 16, "pf": 32, "pd": 32,
+                "dl": 32, "t1": 32, "t2": 32, "fl": 32, "arow": K, "brow": K, "asc": K, "md": K, "hold": K, "aca": 16,
+                "acb": 16, "ace": 16, "rka": 16, "rkb": 16, "kl": 16, "e2": 16, "ef": 16, "af": 16, "prow": C, "yt": C},
+    "int32": {"pi": 8, "pq": 8, "ptl": 28},
+    "uint16": {"qo": 28, "uo": 8, "pu": 32, "lu": 32, "ku": 16, "ru": 16, "eu": 16, "au": 16},
+    CODE: {"qx": C, "qu": 128, "qr": 128, "qw": 512, "qe": 512, "qh": K},
+    "uint8": {"sx": C, "su": 128, "sr": 128, "sw": 512, "se": 512, "sh": K},
+}
+STAGES = [("w", 512)] + [(str(_t), K) for _t in range(R)]
+for _t, _w in STAGES:
+    BUFFERS[CODE].update({"rq" + _t: _w // 2, "lq" + _t: _w})
+    BUFFERS["uint8"].update({"rs" + _t: _w, "ls" + _t: _w})
+SCRATCH = {_n: ("sbuf", [128, _w], _d) for _d in BUFFERS for _n, _w in BUFFERS[_d].items()}
+SCRATCH["ps"] = ("psum", [128, 4096], "float32")
+
+SEMAPHORES = ["cv", "cs", "cp", "cg", "dptr", "du", "dxa", "dxb", "dwc", "dws", "st", "sent"] + \
+    [_n + _t for _t, _w in STAGES for _n in ("out", "hop", "arr")]
+
+OP = AluOpType
+AF = ActivationFunctionType
+BK_A, BK_A2, BK_B, BK_B2 = 4, 5, 6, 7
+
+
+def relays(src, dst, topo):
+    ok = [c for c in topo.cores_of(src) if c != src and topo.may_write(c, dst)]
+    near = [c for c in ok if topo.die(c) == topo.die(src)]
+    far = [c for c in ok if topo.die(c) != topo.die(src)]
+    return near[0], far[0], near[1]
+
+
+def mask_of(engines):
+    m = 0
+    for e in engines:
+        m |= 1 << e
+    return m
+
+
+def relay_program(g, core, T, topo):
+    n = len(T.cores)
+    for r in range(n):
+        src, dst = T.cores[r], T.cores[(r + 1) % n]
+        rl = relays(src, dst, topo)
+        if core not in rl:
+            continue
+        part = rl.index(core)
+        rid, pid = topo.addr(dst, core)
+        m = topo.mask(core, dst)
+        ne = len(topo.engines(core, dst))
+        nin = len(topo.engines(src, core))
+        for t, w in STAGES:
+            if part < 2:
+                g.wait_ge(T.sem["hop" + t], nin // 2)
+                h = w // 2
+                g.remote_dma(T["lq" + t][:, part * h:part * h + h].bitcast(dt.uint8), T["rq" + t][:].bitcast(dt.uint8),
+                             T.sem["arr" + t], T.sem.sent, pid, rid, m)
+            else:
+                g.wait_ge(T.sem["hop" + t], nin)
+                g.remote_dma(T["ls" + t][:], T["rs" + t][:], T.sem["arr" + t], T.sem.sent, pid, rid, m)
+        g.wait_ge(T.sem.sent, len(STAGES) * ne)
+
+
+def clash(a, b):
+    if a[0] != b[0] or a[1] >= b[2] or b[1] >= a[2]:
+        return False
+    return not (a[3] > 1 and a[3] == b[3] and (a[1] - b[1]) % a[3] != 0)
+
+
+def emit(g, T, ops):
+    eng = {"v": g.vector, "s": g.scalar, "p": g.tensor, "g": g, "y": g.sync}
+    csem = {"v": "cv", "s": "cs", "p": "cp", "g": "cg"}
+    deps = []
+    for i, o in enumerate(ops):
+        last = {}
+        for j in range(i - 1, -1, -1):
+            e = ops[j]
+            key = e["sem"] or e["q"]
+            if key in last or e["quiet"]:
+                continue
+            if any(clash(a, b) for a in o["r"] for b in e["w"]) or any(clash(a, b) for a in o["w"] for b in e["w"] + e["r"]) or \
+                    (e["q"] != o["q"] and any(a[0] == "ps" and clash(a, b) for a in o["r"] for b in e["r"])):
+                last[key] = j
+        deps.append(sorted(last.values()))
+    need = set()
+    known = {q: {} for q in eng}
+    clock = {}
+    keep = []
+    for i, o in enumerate(ops):
+        kn = known[o["q"]]
+        w = []
+        for j in reversed(deps[i]):
+            key = ops[j]["sem"] or ops[j]["q"]
+            if kn.get(key, -1) >= j:
+                continue
+            w.append(j)
+            need.add(j)
+            kn[key] = j
+            for k2, v2 in clock[j].items():
+                kn[k2] = max(kn.get(k2, -1), v2)
+        keep.append(w)
+        clock[i] = dict(kn)
+    count, total, waited = {}, {}, {}
+    for i, o in enumerate(ops):
+        q = eng[o["q"]]
+        for j in keep[i]:
+            name, val = count[j]
+            q.wait_ge(T.sem[name], val)
+            waited[name] = max(waited.get(name, 0), val)
+        ins = o["f"](q)
+        if o["sem"] is not None:
+            total[o["sem"]] = total.get(o["sem"], 0) + 16
+            ins.then_inc(T.sem[o["sem"]], 16)
+            count[i] = (o["sem"], total[o["sem"]])
+        elif i in need:
+            name = csem[o["q"]]
+            total[name] = total.get(name, 0) + 1
+            ins.then_inc(T.sem[name], 1)
+            count[i] = (name, total[name])
+    for name in total:
+        if waited.get(name, 0) < total[name]:
+            g.wait_ge(T.sem[name], total[name])
+
+
+def rank_program(g, core, T, topo):
+    rank = T.rank_of(core)
+    if rank is None:
+        relay_program(g, core, T, topo)
+        return
+    n = len(T.cores)
+    nxt, prv = T.cores[(rank + 1) % n], T.cores[(rank - 1) % n]
+    ops = []
+
+    def V(name, lo, hi, step=1):
+        return (name, lo, hi, step)
+
+    def P(bank, lo=0, hi=K):
+        return ("ps", 512 * bank + lo, 512 * bank + hi, 1)
+
+    def ap(v):
+        if not isinstance(v, tuple):
+            return v
+        return T[v[0]][:, v[1]:v[2]:v[3]] if v[3] > 1 else T[v[0]][:, v[1]:v[2]]
+
+    def tr(v):
+        return ("ps", v[1] // 512 * 512, v[1] // 512 * 512 + 512, 1) if v[0] == "ps" else v
+
+    def add(q, f, r, w, sem=None, quiet=False):
+        ops.append({"q": q, "f": f, "r": [tr(v) for v in r if isinstance(v, tuple)], "w": [tr(v) for v in w],
+                    "sem": sem, "quiet": quiet})
+
+    def src(v, off):
+        return ap(v) if off is None else ap(v).indirect(ap(off))
+
+    def copy(out, in_, off=None):
+        add("v", lambda q: q.tensor_copy(ap(out), src(in_, off)), [in_, off], [out])
+
+    def tt(out, a, b, op, off=None):
+        add("v", lambda q: q.tensor_tensor(ap(out), src(a, off), ap(b), op), [a, b, off], [out])
+
+    def ts(out, a, s1, op0, s2=None, op1=None):
+        if op1 is None:
+            add("v", lambda q: q.tensor_scalar(ap(out), ap(a), ap(s1), None, op0), [a, s1], [out])
+        else:
+            add("v", lambda q: q.tensor_scalar(ap(out), ap(a), ap(s1), ap(s2), op0, op1), [a, s1, s2], [out])
+
+    def scan(out, d0, d1, init, op0, op1):
+        add("v", lambda q: q.tensor_tensor_scan(ap(out), ap(d0), ap(d1), init, op0, op1), [d0, d1], [out])
+
+    def fill(out, c):
+        add("v", lambda q: q.memset(ap(out), c), [], [out])
+
+    def act(out, in_, func, off=None, scale=None, bias=None, acc=None):
+        kw = {}
+        if scale is not None:
+            kw["scale"] = scale
+        if bias is not None:
+            kw["bias"] = ap(bias)
+        if acc is not None:
+            kw["accum_out"] = ap(acc)
+        add("s", lambda q: q.activation(ap(out), src(in_, off), func, **kw), [in_, off, bias],
+            [out] + ([acc] if acc is not None else []))
+
+    def quant(c, s, in_):
+        add("v", lambda q: q.quantize_mx(ap(c), ap(s), ap(in_)), [in_], [c, s])
+
+    def mm(out, wc, ws, xc, xs):
+        add("p", lambda q: q.matmul_mx(ap(out), ap(wc), ap(ws), ap(xc), ap(xs), True, True), [wc, ws, xc, xs], [out])
+
+    def dma(qn, out, in_, r, w, sem):
+        add(qn, lambda q: q.dma_start(out, in_), r, w, sem)
+
+    def wait(qn, sem, val):
+        add(qn, lambda q: q.wait_ge(T.sem[sem], val), [], [], quiet=True)
+
+    def to_list(row):
+        w = row[2] - row[1]
+        scan(V("ms", 0, w), V("cap", 0, w), row, 0.0, OP.add, OP.max)
+        return V("ms", 15, w, 16)
+
+    OFF, OFFK, NEG1, NEGK = V("off", 0, 1), V("off", 3, 4), V("off", 4, 5), V("off", 5, 6)
+    UR = (V("qr", 0, 128), V("sr", 0, 128))
+    QA = (V("qx", 0, K), V("sx", 0, K))
+    QB = (V("qx", K, C), V("sx", K, C))
+
+    def pointer_lists(w):
+        tt(V("t1", 0, w), V("pf", 0, w), V("il", 0, w), OP.is_equal)
+        ts(V("t2", 0, w), V("t1", 0, w), float(C), OP.mult)
+        tt(V("pd", 0, w), V("t2", 0, w), V("pf", 0, w), OP.max)
+        tt(V("dl", 0, w), V("il", 0, w), V("pd", 0, w), OP.subtract)
+
+    dma("s", T.ptl[:], T.ptr[:], [], [V("ptl", 0, 28)], "dptr")
+    dma("y", T.xt[:, 0:4 * K], T.x[:, 0:4 * K], [], [V("xt", 0, 4 * K)], "dxa")
+    dma("s", T.ut[:], T.u[:], [], [V("ut", 0, 512)], "du")
+    dma("y", T.xt[:, 4 * K:4 * C], T.x[:, 4 * K:4 * C], [], [V("xt", 4 * K, 4 * C)], "dxb")
+    add("g", lambda q: q.iota(T.pi[:, 0:1], [[0, 1]], 0, 1), [], [V("pi", 0, 1)])
+    add("g", lambda q: q.iota(T.iot[:], [[1, RW]], 0, 0, allow_small_or_imprecise_dtypes=True), [], [V("iot", 0, RW)])
+    fill(V("one", 0, 520), 1.0)
+    add("g", lambda q: q.affine_select(T.et[:, 0:516], T.one[:, 0:516], [[-1, 516]], OP.is_equal, 0.0, 3, 4),
+        [V("one", 0, 516)], [V("et", 0, 516)])
+    for nm in ("ra", "rb", "rc"):
+        fill(V(nm, C, RW), float(C - K))
+    fill(V("asc", 0, K), 0.0)
+    fill(NEG1, -1.0)
+    fill(NEGK, -float(K))
+    ts(V("pq", 0, 1), V("pi", 0, 1), 15, OP.bitwise_and)
+    copy(V("qf", 0, 1), V("pq", 0, 1))
+    Q = V("qf", 0, 1)
+    ts(V("qf", 1, 2), Q, 1.0, OP.add)
+    ts(OFF, Q, 14.5, OP.is_lt, LIFT, OP.mult)
+    ts(V("qo", 0, 28), V("one", 0, 28), Q, OP.mult)
+    ts(OFFK, OFF, float(K), OP.subtract)
+    I16 = V("iot", 0, 16)
+    ts(V("w16", 0, 16), I16, Q, OP.is_equal, -2 * BIG, OP.mult)
+    ts(V("w16", 16, 32), I16, 0.5, OP.is_lt, 2 * BIG, OP.mult)
+    ts(V("w16", 32, 48), I16, Q, OP.is_equal, -2 * LIFT, OP.mult)
+    ts(V("w16", 48, 64), I16, V("qf", 1, 2), OP.is_equal, LIFT, OP.mult)
+    ts(V("w16", 64, 80), I16, 0.5, OP.is_gt)
+    ts(V("w16", 0, 16), V("w16", 0, 16), BIG, OP.add)
+    ts(V("w16", 16, 32), V("w16", 16, 32), BIG, OP.subtract)
+    tt(V("w16", 32, 48), V("w16", 32, 48), V("w16", 48, 64), OP.add)
+    act(V("mk", 0, K), V("w16", 0, 16), AF.Copy, off=V("qo", 0, NK))
+    act(V("rst", 0, K), V("w16", 16, 32), AF.Copy, off=V("qo", 0, NK))
+    act(V("keep", 0, K), V("w16", 64, 80), AF.Copy, off=V("qo", 0, NK))
+    act(V("cap", 0, C), V("w16", 32, 48), AF.Copy, off=V("qo", 0, 28))
+    act(V("iom", 0, RW), V("iot", 0, RW), AF.Identity, bias=NEGK)
+    copy(V("uo", 0, 8), V("iot", 0, 128, 16))
+    ts(V("il", 0, 28), V("iot", 0, C, 16), Q, OP.add)
+    ts(V("nl", 0, NK), V("iot", 0, K, 16), Q, OP.add, 0.5, OP.add)
+    ts(V("c2", 0, NK), V("iot", 0, K, 16), 2.0, OP.mult, float(FW), OP.add)
+    copy(V("pf", 0, 28), V("ptl", 0, 28))
+    copy(V("pu", 0, 28), V("ptl", 0, 28))
+    pointer_lists(28)
+    quant(V("qu", 0, 128), V("su", 0, 128), V("ut", 0, 512))
+    add("v", lambda q: q.tensor_copy(T.qr[:, 0:128].bitcast(dt.uint32), T.qu[:, 0:128].bitcast(dt.uint32).indirect(T.uo[:, 0:8])),
+        [V("qu", 0, 128), V("uo", 0, 8)], [V("qr", 0, 128)])
+    copy(V("sr", 0, 128), V("su", 0, 128), V("uo", 0, 8))
+
+    def unit_tiles(bs):
+        for b in bs:
+            quant(V("qe", 128 * b, 128 * b + 128), V("se", 128 * b, 128 * b + 128), V("et", 3 - b, 515 - b))
+
+    def planes(lo, hi):
+        for b in range(4):
+            act(V("xh", C * b + lo, C * b + hi), V("xt", 4 * lo + b, 4 * hi, 4), AF.Copy, scale=0.5)
+
+    def ranks(bank, fn, an, rn, between=None):
+        tt(V("md", 0, K), P(bank), V("mk", 0, K), OP.max)
+        scan(V("hold", 0, K), V("rst", 0, K), V("md", 0, K), BIG, OP.max, OP.min)
+        for k in range(NK):
+            s, c = V("hold", 16 * k + 15, 16 * k + 16), 16 * k + 16
+            ts(V(fn, K * k, K * k + c), P(bank, 0, c), s, OP.is_ge)
+            if c < K:
+                ts(V(fn, K * k + c, K * k + K), P(bank, c, K), s, OP.is_gt)
+            act(V(fn, K * k, K * k + K), V(fn, K * k, K * k + K), AF.Copy, acc=V(an, k, k + 1))
+            if between is not None:
+                between(k)
+        tt(V("eq", 0, K), P(bank), V("hold", 0, K), OP.is_equal)
+        scan(V("es", 0, K), V("keep", 0, K), V("eq", 0, K), 0.0, OP.mult, OP.add)
+        tt(V(rn, 0, NK), V(an, 0, NK), V("es", 15, K, 16), OP.subtract)
+
+    def sort_a():
+        ts(V("ku", 0, NK), V("rka", 0, NK), -1.0, OP.mult, float(K - 1), OP.add)
+        ts(V("kl", 0, NK), V("rka", 0, NK), -1.0, OP.mult, float(K - 1), OP.add)
+        add("v", lambda q: q.tensor_copy(T.asc[:, 0:K].indirect(T.ku[:, 0:NK]), T.arow[:, 0:K]),
+            [V("arow", 0, K), V("ku", 0, NK)], [V("asc", 0, K)])
+        act(V("krow", 0, K), V("iot", 0, K), AF.Copy, off=V("ku", 0, NK))
+
+    def count_e(ks):
+        for k in ks:
+            act(V("junk", FW * k, FW * k + FW), V("cum", 16 * k, 16 * k + FW), AF.Sign, scale=-1.0,
+                bias=V("nl", k, k + 1), acc=V("ace", k, k + 1))
+
+    def select():
+        copy(V("ru", 0, NK), V("rkb", 0, NK))
+        tt(V("f", K, C), V("asc", 0, K), V("brow", 0, K), OP.is_lt, off=V("ru", 0, NK))
+        scan(V("cb", 0, K), V("one", 0, K), V("f", K, C), 0.0, OP.mult, OP.add)
+        ts(V("f", 0, K), V("krow", 0, K), V("cb", K - 1, K), OP.is_ge)
+
+    def both(out, win, lst, nv):
+        copy(V(out[0], out[1], out[1] + 16 * nv), win, V(lst[0], lst[1], lst[1] + nv))
+        if lst[1] + nv < lst[2]:
+            act(V(out[0], out[1] + 16 * nv, out[2]), win, AF.Copy, off=V(lst[0], lst[1] + nv, lst[2]))
+
+    def climb(w):
+        nw, share, split = w // 16, SHARE[w], SPLIT[w]
+        nb = V("cb", K - 1, K)
+        ts(V("fl", 0, NK), V("kl", 0, NK), nb, OP.is_ge)
+        if w == C:
+            ts(V("fl", NK, 2 * NK), V("rkb", 0, NK), nb, OP.is_lt)
+        scan(V("cum", 0, C), V("one", 0, C), V("f", 0, C), 0.0, OP.mult, OP.add)
+        tt(V("t1", 0, nw), V("fl", 0, nw), V("dl", 0, nw), OP.mult)
+        tt(V("t2", 0, nw), V("t1", 0, nw), V("pd", 0, nw), OP.add)
+        L = V("lu", 0, nw)
+        copy(L, V("t2", 0, nw))
+        a, b, c = "ra", "rb", "rc"
+        count_e(range(0, share[0]))
+        done = share[0]
+        both(V(a, 0, w), V("iom", 0, RW), L, split[0])
+        for s in range(5):
+            both(V(b, 0, w), V(a, 0, RW), L, split[2] if s else split[1])
+            if s == 4:
+                tt(V("e2", 0, NK), V("ace", 0, NK), V("c2", 0, NK), OP.add)
+            both(V(c, 0, w) if s < 4 or w == C else V("exb", K, C), V(b, 0, RW), L, split[3])
+            if s < 4:
+                count_e(range(done, done + share[s + 1]))
+                done += share[s + 1]
+                ts(L, to_list(V(c, 0, w)), OFFK, OP.subtract)
+                a, b, c = c, a, b
+        ts(V("eu", 0, NK), V("e2", 0, NK), 0.5, OP.mult)
+        ts(V("ef", 0, NK), V("e2", 0, NK), 0.5, OP.mult, OFFK, OP.add)
+        if w == C:
+            both(V("exb", 0, C), V(c, 0, RW), V("pu", 0, nw), split[3])
+        else:
+            both(V("exb", 0, K), V("exb", K, C), V("pu", 0, nw), NH)
+        both(V("xr", 0, K), V("exb", 0, C), V("eu", 0, NK), NH)
+        for b in range(4):
+            act(V("vh", K * b, K * b + K), V("xh", C * b, C * b + C), AF.Copy, off=V("eu", 0, NK))
+        tt(V("af", 0, NK), to_list(V("xr", 0, K)), V("ef", 0, NK), OP.min)
+        ts(V("au", 0, NK), V("af", 0, NK), OFFK, OP.subtract)
+
+    rl = relays(core, nxt, topo)
+    en = topo.engines(core, rl[0])
+    landed = sum(len(topo.engines(c, core)) for c in relays(prv, core, topo))
+
+    def send(t, qn, sn, w):
+        h, half = w // 2, len(en) // 2
+
+        def calls(q):
+            trs = []
+            for i in range(2):
+                rid, pid = topo.addr(rl[i], core)
+                trs.append(RemoteDMATransfer(dst_ids=[DstId(rid=rid, pnc=pid)], dma_engine_mask=mask_of(en[i * half:i * half + half]),
+                                             remote_sem=T.sem["hop" + t], src=T[qn][:, i * h:i * h + h].bitcast(dt.uint8),
+                                             dst=T["rq" + t][:].bitcast(dt.uint8)))
+            q.remote_dma_fused(trs, local_sem=T.sem["out" + t])
+            rid, pid = topo.addr(rl[2], core)
+            q.remote_dma(T["rs" + t][:], T[sn][:, 0:w], T.sem["hop" + t], T.sem["out" + t], pid, rid, mask_of(en))
+        add("g", calls, [V(qn, 0, w), V(sn, 0, w)], [], quiet=True)
+
+    def blend(t):
+        for b in range(4):
+            tt(V("xt", b, 4 * K, 4), V("xh", C * b, C * b + C), V("vh", K * b, K * b + K), OP.add, off=V("au", 0, NK))
+            if t > 0 and b == 0:
+                wait("v", "out%d" % (t - 1), 2 * len(en))
+        quant(QA[0], QA[1], V("xt", 0, 4 * K))
+        send(str(t), "qx", "sx", K)
+
+    def arrive(t):
+        if t == 0:
+            wait("p", "arrw", landed)
+        wait("p", "arr%d" % t, landed)
+        for b in range(4):
+            mm(P(b), V("lqw", 128 * b, 128 * b + 128), V("lsw", 128 * b, 128 * b + 128), V("lq%d" % t, 0, K), V("ls%d" % t, 0, K))
+        for b in range(4):
+            if b % 2 == 0:
+                act(V("ht", b, 4 * K, 4), P(b), AF.Relu, scale=0.03125)
+            else:
+                ts(V("ht", b, 4 * K, 4), P(b), 0.0, OP.max, 0.03125, OP.mult)
+        quant(V("qh", 0, K), V("sh", 0, K), V("ht", 0, 4 * K))
+        for b in range(4):
+            mm(P(b), V("qe", 128 * b, 128 * b + 128), V("se", 128 * b, 128 * b + 128), V("qh", 0, K), V("sh", 0, K))
+        for b in range(4):
+            if b % 2 == 0:
+                act(V("xt", 4 * K + b, 4 * C, 4), P(b), AF.Copy)
+            else:
+                copy(V("xt", 4 * K + b, 4 * C, 4), P(b))
+        quant(QB[0], QB[1], V("xt", 4 * K, 4 * C))
+
+    unit_tiles([0, 1])
+    quant(QA[0], QA[1], V("xt", 0, 4 * K))
+    mm(P(BK_A), UR[0], UR[1], QA[0], QA[1])
+    mm(P(BK_A2), UR[0], UR[1], QA[0], QA[1])
+    dma("y", T.qw[:].bitcast(dt.uint8), T.wc[:], [], [V("qw", 0, 512)], "dwc")
+    dma("y", T.sw[:], T.ws[:], [], [V("sw", 0, 512)], "dws")
+    send("w", "qw", "sw", 512)
+    unit_tiles([2, 3])
+    planes(0, K)
+    act(V("arow", 0, K), P(BK_A2), AF.Copy)
+
+    def second_half(k):
+        if k == 6:
+            quant(QB[0], QB[1], V("xt", 4 * K, 4 * C))
+            mm(P(BK_B), UR[0], UR[1], QB[0], QB[1])
+            mm(P(BK_B2), UR[0], UR[1], QB[0], QB[1])
+
+    ranks(BK_A, "fa", "aca", "rka", second_half)
+    act(V("brow", 0, K), P(BK_B2), AF.Copy)
+    ranks(BK_B, "fb", "acb", "rkb", lambda k: sort_a() if k == NK - 1 else None)
+    planes(K, C)
+    for t in range(R):
+        select()
+        climb(C if t == 0 else K)
+        blend(t)
+        if t < R - 1:
+            act(V("pr", 0, K), V("cum", 0, C), AF.Identity, off=V("au", 0, NK), bias=NEG1)
+            mm(P(BK_A), UR[0], UR[1], QA[0], QA[1])
+            mm(P(BK_A2), UR[0], UR[1], QA[0], QA[1])
+            lst = to_list(V("pr", 0, K))
+            ts(V("pf", 0, NK), lst, OFF, OP.subtract)
+            ts(V("pu", 0, NK), lst, OFF, OP.subtract)
+            act(V("arow", 0, K), P(BK_A2), AF.Copy)
+            ranks(BK_A, "fa", "aca", "rka")
+            sort_a()
+            pointer_lists(NK)
+            planes(0, K)
+            arrive(t)
+            mm(P(BK_B), UR[0], UR[1], QB[0], QB[1])
+            mm(P(BK_B2), UR[0], UR[1], QB[0], QB[1])
+            planes(K, C)
+            act(V("brow", 0, K), P(BK_B2), AF.Copy)
+            ranks(BK_B, "fb", "acb", "rkb")
+        else:
+            mm(P(BK_A), V("qu", 0, 128), V("su", 0, 128), QA[0], QA[1])
+            dma("y", T.oc[:, 0:4 * K], T.qx[:, 0:K].bitcast(dt.uint8), [QA[0]], [], "st")
+            act(V("prow", 0, K), V("cum", 0, C), AF.Identity, off=V("au", 0, NK), bias=NEG1)
+            copy(V("prow", K, C), V("iot", 0, K))
+            copy(V("yt", 0, K), P(BK_A))
+            dma("y", T.pl[:], T.prow[0:128:16, :], [V("prow", 0, C)], [], "st")
+            dma("y", T.y[:, 0:K], T.yt[:, 0:K], [V("yt", 0, K)], [], "st")
+            arrive(t)
+            mm(P(BK_B), V("qu", 0, 128), V("su", 0, 128), QB[0], QB[1])
+            dma("y", T.oc[:, 4 * K:4 * C], T.qx[:, K:C].bitcast(dt.uint8), [QB[0]], [], "st")
+            for k in range(4):
+                dma("y" if k < 2 else "s", T.osc[4 * k:4 * k + 4, :], T.sx[32 * k:32 * k + 4, :], [V("sx", 0, C)], [], "st")
+            copy(V("yt", K, C), P(BK_B))
+            dma("s", T.y[:, K:C], T.yt[:, K:C], [V("yt", K, C)], [], "st")
+    emit(g, T, ops)
+    for t in ("w", str(R - 1)):
+        g.wait_ge(T.sem["out" + t], 2 * len(en))

@@ -6,21 +6,23 @@ FW = K + 16
 RW = C + 16
 BIG = 1e29
 LIFT = 1024.0
-SHARE = {C: [2, 3, 3, 3, 3], K: [3, 3, 3, 3, 2]}
-SPLIT = {C: [14, 14, 20, 14], K: [14, 14, 14, 8]}
-NH = 8
+NV = 8
+STEPS = 9
+SPLIT = {C: 6, K: 0}
+SHARE = {C: [3, 2, 2, 2, 2, 2, 1, 0, 0, 0, 0], K: [3, 2, 2, 2, 2, 2, 1, 0, 0, 0, 0]}
 CODE = "float8_e4m3fn_x4"
 
 BUFFERS = {
     "bfloat16": {"xt": 4 * C, "xh": 4 * C, "ut": 512, "ht": 4 * K, "vh": 4 * K, "et": 520, "one": 520, "iom": RW,
                  "cap": C, "keep": K, "fa": NK * K, "fb": NK * K, "junk": NK * FW, "eq": K, "es": K, "krow": K, "f": C,
-                 "cb": K, "cum": C, "ra": RW, "rb": RW, "rc": RW, "pr": K, "exb": C, "xr": K},
-    "float16": {"ms": C},
-    "float32": {"iot": RW, "w16": 80, "off": 8, "qf": 8, "mk": K, "rst": K, "il": 32, "nl": 16, "c2": 16, "pf": 32, "pd": 32,
+                 "cb": K, "cum": C, "ra": RW, "rb": RW, "rc": RW, "pr": C, "exb": K, "xr": K, "xp": K, "sm": NK * FW // 2},
+    "float16": {"ms": C, "ms2": K},
+    "float32": {"iot": RW, "w16": 80, "off": 8, "qf": 8, "mk": K, "rst": K, "il": 32, "nl": 16, "pf": 32, "pd": 32,
                 "dl": 32, "t1": 32, "t2": 32, "fl": 32, "arow": K, "brow": K, "asc": K, "md": K, "hold": K, "aca": 16,
-                "acb": 16, "ace": 16, "rka": 16, "rkb": 16, "kl": 16, "e2": 16, "ef": 16, "af": 16, "prow": C, "yt": C},
+                "acb": 16, "rka": 16, "rkb": 16, "kl": 16, "e2": 16, "gl": 16, "esc": 16, "cc": 16, "ef": 16, "af": 16,
+                "prow": C, "yt": C},
     "int32": {"pi": 8, "pq": 8, "ptl": 28},
-    "uint16": {"qo": 28, "uo": 8, "pu": 32, "lu": 32, "ku": 16, "ru": 16, "eu": 16, "au": 16},
+    "uint16": {"qo": 28, "uo": 8, "pu": 32, "lu": 64, "pe": 16, "yl": 16, "ku": 16, "ru": 16, "eu": 16, "au": 16},
     CODE: {"qx": C, "qu": 128, "qr": 128, "qw": 512, "qe": 512, "qh": K},
     "uint8": {"sx": C, "su": 128, "sr": 128, "sw": 512, "se": 512, "sh": K},
 }
@@ -209,12 +211,12 @@ def rank_program(g, core, T, topo):
     def wait(qn, sem, val):
         add(qn, lambda q: q.wait_ge(T.sem[sem], val), [], [], quiet=True)
 
-    def to_list(row):
+    def to_list(row, ms="ms"):
         w = row[2] - row[1]
-        scan(V("ms", 0, w), V("cap", 0, w), row, 0.0, OP.add, OP.max)
-        return V("ms", 15, w, 16)
+        scan(V(ms, 0, w), V("cap", 0, w), row, 0.0, OP.add, OP.max)
+        return V(ms, 15, w, 16)
 
-    OFF, OFFK, NEG1, NEGK = V("off", 0, 1), V("off", 3, 4), V("off", 4, 5), V("off", 5, 6)
+    OFF, OFFK, NEG1, NEGK, NEGK1 = V("off", 0, 1), V("off", 3, 4), V("off", 4, 5), V("off", 5, 6), V("off", 6, 7)
     UR = (V("qr", 0, 128), V("sr", 0, 128))
     QA = (V("qx", 0, K), V("sx", 0, K))
     QB = (V("qx", K, C), V("sx", K, C))
@@ -237,8 +239,10 @@ def rank_program(g, core, T, topo):
     for nm in ("ra", "rb", "rc"):
         fill(V(nm, C, RW), float(C - K))
     fill(V("asc", 0, K), 0.0)
+    fill(V("gl", 0, 16), 0.0)
     fill(NEG1, -1.0)
     fill(NEGK, -float(K))
+    fill(NEGK1, -float(K + 1))
     ts(V("pq", 0, 1), V("pi", 0, 1), 15, OP.bitwise_and)
     copy(V("qf", 0, 1), V("pq", 0, 1))
     Q = V("qf", 0, 1)
@@ -258,19 +262,18 @@ def rank_program(g, core, T, topo):
     act(V("mk", 0, K), V("w16", 0, 16), AF.Copy, off=V("qo", 0, NK))
     act(V("rst", 0, K), V("w16", 16, 32), AF.Copy, off=V("qo", 0, NK))
     act(V("keep", 0, K), V("w16", 64, 80), AF.Copy, off=V("qo", 0, NK))
-    act(V("cap", 0, C), V("w16", 32, 48), AF.Copy, off=V("qo", 0, 28))
-    act(V("iom", 0, RW), V("iot", 0, RW), AF.Identity, bias=NEGK)
-    copy(V("uo", 0, 8), V("iot", 0, 128, 16))
-    ts(V("il", 0, 28), V("iot", 0, C, 16), Q, OP.add)
-    ts(V("nl", 0, NK), V("iot", 0, K, 16), Q, OP.add, 0.5, OP.add)
-    ts(V("c2", 0, NK), V("iot", 0, K, 16), 2.0, OP.mult, float(FW), OP.add)
-    copy(V("pf", 0, 28), V("ptl", 0, 28))
-    copy(V("pu", 0, 28), V("ptl", 0, 28))
-    pointer_lists(28)
     quant(V("qu", 0, 128), V("su", 0, 128), V("ut", 0, 512))
+    copy(V("uo", 0, 8), V("iot", 0, 128, 16))
     add("v", lambda q: q.tensor_copy(T.qr[:, 0:128].bitcast(dt.uint32), T.qu[:, 0:128].bitcast(dt.uint32).indirect(T.uo[:, 0:8])),
         [V("qu", 0, 128), V("uo", 0, 8)], [V("qr", 0, 128)])
     copy(V("sr", 0, 128), V("su", 0, 128), V("uo", 0, 8))
+
+    def later_constants():
+        copy(V("pf", 0, 28), V("ptl", 0, 28))
+        copy(V("pu", 0, 28), V("ptl", 0, 28))
+        ts(V("il", 0, 28), V("iot", 0, C, 16), Q, OP.add)
+        ts(V("nl", 0, NK), V("iot", 0, K, 16), Q, OP.add, 0.5, OP.add)
+        pointer_lists(28)
 
     def unit_tiles(bs):
         for b in bs:
@@ -280,78 +283,131 @@ def rank_program(g, core, T, topo):
         for b in range(4):
             act(V("xh", C * b + lo, C * b + hi), V("xt", 4 * lo + b, 4 * hi, 4), AF.Copy, scale=0.5)
 
-    def ranks(bank, fn, an, rn, between=None):
+    def ranks(bank, row, fn, an, rn, between=None):
+        H = K // 2
         tt(V("md", 0, K), P(bank), V("mk", 0, K), OP.max)
         scan(V("hold", 0, K), V("rst", 0, K), V("md", 0, K), BIG, OP.max, OP.min)
-        for k in range(NK):
+        for k in range(NV, NK):
+            act(V(fn, K * k, K * k + K), V(row, 0, K), AF.Sign, scale=-1.0, bias=V("hold", 16 * k + 15, 16 * k + 16))
+        for k in range(NV, NK - 1):
+            c = 16 * k + 16
+            act(V(fn, K * k + c, K * k + K), V(fn, K * k + c, K * k + K), AF.Relu, scale=-1.0, acc=V("gl", k, k + 1))
+        for k in range(NV, NK):
+            c = 16 * k + 16
+            act(V(fn, K * k, K * k + c), V(fn, K * k, K * k + c), AF.Relu, acc=V(an, k, k + 1))
+
+        def total(k):
+            scan(V("sm", H * k, H * k + H), V(fn, K * k, K * k + H), V(fn, K * k + H, K * k + K), 0.0, OP.add, OP.add)
+        for k in range(NV):
             s, c = V("hold", 16 * k + 15, 16 * k + 16), 16 * k + 16
             ts(V(fn, K * k, K * k + c), P(bank, 0, c), s, OP.is_ge)
-            if c < K:
-                ts(V(fn, K * k + c, K * k + K), P(bank, c, K), s, OP.is_gt)
-            act(V(fn, K * k, K * k + K), V(fn, K * k, K * k + K), AF.Copy, acc=V(an, k, k + 1))
+            ts(V(fn, K * k + c, K * k + K), P(bank, c, K), s, OP.is_gt)
+            if k > 0:
+                total(k - 1)
+            if k == NV - 2:
+                tt(V("eq", 0, K), P(bank), V("hold", 0, K), OP.is_equal)
             if between is not None:
                 between(k)
-        tt(V("eq", 0, K), P(bank), V("hold", 0, K), OP.is_equal)
         scan(V("es", 0, K), V("keep", 0, K), V("eq", 0, K), 0.0, OP.mult, OP.add)
-        tt(V(rn, 0, NK), V(an, 0, NK), V("es", 15, K, 16), OP.subtract)
+        tt(V("esc", NV, NK), V("cc", NV, NK), V("gl", NV, NK), OP.add)
+        total(NV - 1)
+        tt(V("esc", NV, NK), V("esc", NV, NK), V("es", 16 * NV + 15, K, 16), OP.subtract)
+        tt(V(rn, 0, NV), V("sm", H - 1, H * NV, H), V("es", 15, 16 * NV, 16), OP.subtract)
+        tt(V(rn, NV, NK), V("esc", NV, NK), V(an, NV, NK), OP.subtract)
 
     def sort_a():
         ts(V("ku", 0, NK), V("rka", 0, NK), -1.0, OP.mult, float(K - 1), OP.add)
         ts(V("kl", 0, NK), V("rka", 0, NK), -1.0, OP.mult, float(K - 1), OP.add)
         add("v", lambda q: q.tensor_copy(T.asc[:, 0:K].indirect(T.ku[:, 0:NK]), T.arow[:, 0:K]),
             [V("arow", 0, K), V("ku", 0, NK)], [V("asc", 0, K)])
+
+    def rank_row():
         act(V("krow", 0, K), V("iot", 0, K), AF.Copy, off=V("ku", 0, NK))
 
     def count_e(ks):
         for k in ks:
-            act(V("junk", FW * k, FW * k + FW), V("cum", 16 * k, 16 * k + FW), AF.Sign, scale=-1.0,
-                bias=V("nl", k, k + 1), acc=V("ace", k, k + 1))
+            ts(V("junk", FW * k, FW * k + FW), V("cum", 16 * k, 16 * k + FW), V("nl", k, k + 1), OP.is_lt)
+
+    def total_e(ks):
+        h = FW // 2
+        for k in ks:
+            scan(V("sm", h * k, h * k + h), V("junk", FW * k, FW * k + h), V("junk", FW * k + h, FW * k + FW), 0.0, OP.add, OP.add)
 
     def select():
         copy(V("ru", 0, NK), V("rkb", 0, NK))
         tt(V("f", K, C), V("asc", 0, K), V("brow", 0, K), OP.is_lt, off=V("ru", 0, NK))
         scan(V("cb", 0, K), V("one", 0, K), V("f", K, C), 0.0, OP.mult, OP.add)
-        ts(V("f", 0, K), V("krow", 0, K), V("cb", K - 1, K), OP.is_ge)
 
     def both(out, win, lst, nv):
-        copy(V(out[0], out[1], out[1] + 16 * nv), win, V(lst[0], lst[1], lst[1] + nv))
+        if nv:
+            copy(V(out[0], out[1], out[1] + 16 * nv), win, V(lst[0], lst[1], lst[1] + nv))
         if lst[1] + nv < lst[2]:
             act(V(out[0], out[1] + 16 * nv, out[2]), win, AF.Copy, off=V(lst[0], lst[1] + nv, lst[2]))
 
     def climb(w):
-        nw, share, split = w // 16, SHARE[w], SPLIT[w]
+        nw, share, nv = w // 16, SHARE[w], SPLIT[w]
         nb = V("cb", K - 1, K)
+        EU = V("eu", 0, NK)
         ts(V("fl", 0, NK), V("kl", 0, NK), nb, OP.is_ge)
         if w == C:
             ts(V("fl", NK, 2 * NK), V("rkb", 0, NK), nb, OP.is_lt)
-        scan(V("cum", 0, C), V("one", 0, C), V("f", 0, C), 0.0, OP.mult, OP.add)
+        ts(V("f", 0, K), V("krow", 0, K), nb, OP.is_ge)
         tt(V("t1", 0, nw), V("fl", 0, nw), V("dl", 0, nw), OP.mult)
+        scan(V("cum", 0, C), V("one", 0, C), V("f", 0, C), 0.0, OP.mult, OP.add)
         tt(V("t2", 0, nw), V("t1", 0, nw), V("pd", 0, nw), OP.add)
-        L = V("lu", 0, nw)
-        copy(L, V("t2", 0, nw))
-        a, b, c = "ra", "rb", "rc"
-        count_e(range(0, share[0]))
-        done = share[0]
-        both(V(a, 0, w), V("iom", 0, RW), L, split[0])
-        for s in range(5):
-            both(V(b, 0, w), V(a, 0, RW), L, split[2] if s else split[1])
-            if s == 4:
-                tt(V("e2", 0, NK), V("ace", 0, NK), V("c2", 0, NK), OP.add)
-            both(V(c, 0, w) if s < 4 or w == C else V("exb", K, C), V(b, 0, RW), L, split[3])
-            if s < 4:
-                count_e(range(done, done + share[s + 1]))
-                done += share[s + 1]
-                ts(L, to_list(V(c, 0, w)), OFFK, OP.subtract)
-                a, b, c = c, a, b
-        ts(V("eu", 0, NK), V("e2", 0, NK), 0.5, OP.mult)
-        ts(V("ef", 0, NK), V("e2", 0, NK), 0.5, OP.mult, OFFK, OP.add)
-        if w == C:
-            both(V("exb", 0, C), V(c, 0, RW), V("pu", 0, nw), split[3])
-        else:
-            both(V("exb", 0, K), V("exb", K, C), V("pu", 0, nw), NH)
-        both(V("xr", 0, K), V("exb", 0, C), V("eu", 0, NK), NH)
-        for b in range(4):
-            act(V("vh", K * b, K * b + K), V("xh", C * b, C * b + C), AF.Copy, off=V("eu", 0, NK))
+        L = [V("lu", 0, nw), V("lu", 32, 32 + nw)]
+        rows = ["ra", "rb", "rc"]
+        st = {"count": 0, "total": 0, "tail": 0}
+
+        def totals():
+            if st["total"] < st["count"]:
+                total_e(range(st["total"], st["count"]))
+                st["total"] = st["count"]
+            elif st["tail"] == 1:
+                copy(V("xp", 0, K), V("pr", 0, C), EU)
+                st["tail"] = 2
+            elif st["tail"] == 3:
+                ts(V("pe", 0, NK), V("ms2", 15, K, 16), OFFK, OP.subtract)
+                st["tail"] = 4
+
+        def counts(s):
+            count_e(range(st["count"], st["count"] + share[s]))
+            st["count"] += share[s]
+            if st["total"] == NK and st["tail"] == 0:
+                tt(V("e2", 0, NK), V("sm", FW // 2 - 1, NK * FW // 2, FW // 2), V("iot", 0, K, 16), OP.add)
+                copy(EU, V("e2", 0, NK))
+                st["tail"] = 1
+            elif st["tail"] == 2:
+                to_list(V("xp", 0, K), "ms2")
+                st["tail"] = 3
+
+        count_e([0])
+        copy(L[0], V("t2", 0, nw))
+        both(V(rows[0], 0, w), V("iom", 0, RW), L[0], nv)
+        count_e(range(1, share[0]))
+        st["count"] = share[0]
+        both(V(rows[1], 0, w), V(rows[0], 0, RW), L[0], nv)
+        totals()
+        counts(1)
+        for s in range(1, STEPS + 1):
+            a, b = rows[s % 3], rows[(s + 1) % 3]
+            both(V(b, 0, w), V(a, 0, RW), L[(s - 1) % 2], nv)
+            if s < STEPS:
+                lst = to_list(V(a, 0, w))
+                totals()
+                ts(L[s % 2], lst, OFFK, OP.subtract)
+                counts(s + 1)
+        while st["tail"] < 4:
+            totals()
+            counts(len(share) - 1)
+        copy(V("exb", 0, K), V(a, 0, RW), V("pe", 0, NK))
+        lst = to_list(V("exb", 0, K))
+        ts(V("ef", 0, NK), V("e2", 0, NK), OFFK, OP.add)
+        ts(V("yl", 0, NK), lst, OFFK, OP.subtract)
+        for p in range(4):
+            if p == 1:
+                both(V("xr", 0, K), V(b, 0, RW), V("yl", 0, NK), NK)
+            act(V("vh", K * p, K * p + K), V("xh", C * p, C * p + C), AF.Copy, off=EU)
         tt(V("af", 0, NK), to_list(V("xr", 0, K)), V("ef", 0, NK), OP.min)
         ts(V("au", 0, NK), V("af", 0, NK), OFFK, OP.subtract)
 
@@ -382,7 +438,7 @@ def rank_program(g, core, T, topo):
         quant(QA[0], QA[1], V("xt", 0, 4 * K))
         send(str(t), "qx", "sx", K)
 
-    def arrive(t):
+    def arrive(t, gap=None):
         if t == 0:
             wait("p", "arrw", landed)
         wait("p", "arr%d" % t, landed)
@@ -394,6 +450,8 @@ def rank_program(g, core, T, topo):
             else:
                 ts(V("ht", b, 4 * K, 4), P(b), 0.0, OP.max, 0.03125, OP.mult)
         quant(V("qh", 0, K), V("sh", 0, K), V("ht", 0, 4 * K))
+        if gap is not None:
+            gap()
         for b in range(4):
             mm(P(b), V("qe", 128 * b, 128 * b + 128), V("se", 128 * b, 128 * b + 128), V("qh", 0, K), V("sh", 0, K))
         for b in range(4):
@@ -403,49 +461,60 @@ def rank_program(g, core, T, topo):
                 copy(V("xt", 4 * K + b, 4 * C, 4), P(b))
         quant(QB[0], QB[1], V("xt", 4 * K, 4 * C))
 
-    unit_tiles([0, 1])
     quant(QA[0], QA[1], V("xt", 0, 4 * K))
     mm(P(BK_A), UR[0], UR[1], QA[0], QA[1])
     mm(P(BK_A2), UR[0], UR[1], QA[0], QA[1])
+    ts(V("cc", 0, NK), V("iot", 0, K, 16), 16.0, OP.add)
     dma("y", T.qw[:].bitcast(dt.uint8), T.wc[:], [], [V("qw", 0, 512)], "dwc")
     dma("y", T.sw[:], T.ws[:], [], [V("sw", 0, 512)], "dws")
     send("w", "qw", "sw", 512)
-    unit_tiles([2, 3])
-    planes(0, K)
     act(V("arow", 0, K), P(BK_A2), AF.Copy)
 
     def second_half(k):
-        if k == 6:
+        if k == 3:
             quant(QB[0], QB[1], V("xt", 4 * K, 4 * C))
             mm(P(BK_B), UR[0], UR[1], QB[0], QB[1])
             mm(P(BK_B2), UR[0], UR[1], QB[0], QB[1])
 
-    ranks(BK_A, "fa", "aca", "rka", second_half)
+    ranks(BK_A, "arow", "fa", "aca", "rka", second_half)
     act(V("brow", 0, K), P(BK_B2), AF.Copy)
-    ranks(BK_B, "fb", "acb", "rkb", lambda k: sort_a() if k == NK - 1 else None)
+    sort_a()
+    act(V("iom", 0, RW), V("iot", 0, RW), AF.Identity, bias=NEGK)
+    rank_row()
+    act(V("cap", 0, C), V("w16", 32, 48), AF.Copy, off=V("qo", 0, 28))
+    ranks(BK_B, "brow", "fb", "acb", "rkb", lambda k: later_constants() if k == NV - 1 else None)
+    act(V("pr", 0, C), V("iom", 0, RW), AF.Copy, off=V("pu", 0, 28))
+    planes(0, K)
     planes(K, C)
     for t in range(R):
         select()
         climb(C if t == 0 else K)
         blend(t)
         if t < R - 1:
-            act(V("pr", 0, K), V("cum", 0, C), AF.Identity, off=V("au", 0, NK), bias=NEG1)
             mm(P(BK_A), UR[0], UR[1], QA[0], QA[1])
             mm(P(BK_A2), UR[0], UR[1], QA[0], QA[1])
-            lst = to_list(V("pr", 0, K))
-            ts(V("pf", 0, NK), lst, OFF, OP.subtract)
-            ts(V("pu", 0, NK), lst, OFF, OP.subtract)
+            act(V("pr", 0, K), V("cum", 0, C), AF.Identity, off=V("au", 0, NK), bias=NEGK1)
             act(V("arow", 0, K), P(BK_A2), AF.Copy)
-            ranks(BK_A, "fa", "aca", "rka")
-            sort_a()
-            pointer_lists(NK)
+            if t == 0:
+                unit_tiles([0, 1])
+            ranks(BK_A, "arow", "fa", "aca", "rka")
             planes(0, K)
-            arrive(t)
+            if t == 0:
+                unit_tiles([2, 3])
+            sort_a()
+
+            def gap():
+                rank_row()
+                ts(V("pf", 0, NK), to_list(V("pr", 0, K)), OFFK, OP.subtract)
+                if t == 0:
+                    copy(V("pr", K, C), V("iom", 0, K))
+            arrive(t, gap)
             mm(P(BK_B), UR[0], UR[1], QB[0], QB[1])
             mm(P(BK_B2), UR[0], UR[1], QB[0], QB[1])
-            planes(K, C)
+            pointer_lists(NK)
             act(V("brow", 0, K), P(BK_B2), AF.Copy)
-            ranks(BK_B, "fb", "acb", "rkb")
+            ranks(BK_B, "brow", "fb", "acb", "rkb")
+            planes(K, C)
         else:
             mm(P(BK_A), V("qu", 0, 128), V("su", 0, 128), QA[0], QA[1])
             dma("y", T.oc[:, 0:4 * K], T.qx[:, 0:K].bitcast(dt.uint8), [QA[0]], [], "st")

@@ -6,9 +6,9 @@ FW = K + 16
 RW = C + 16
 BIG = 1e29
 LIFT = 1024.0
-NV = 8
+NV = {"a0": 8, "b0": 6, "a": 8, "b": 8}
 STEPS = 9
-SPLIT = {C: 6, K: 0}
+SPLIT = {C: 4, K: 0}
 SHARE = {C: [3, 2, 2, 2, 2, 2, 1, 0, 0, 0, 0], K: [3, 2, 2, 2, 2, 2, 1, 0, 0, 0, 0]}
 CODE = "float8_e4m3fn_x4"
 
@@ -18,8 +18,8 @@ BUFFERS = {
                  "cb": K, "cum": C, "ra": RW, "rb": RW, "rc": RW, "pr": C, "exb": K, "xr": K, "xp": K, "sm": NK * FW // 2},
     "float16": {"ms": C, "ms2": K},
     "float32": {"iot": RW, "w16": 80, "off": 8, "qf": 8, "mk": K, "rst": K, "il": 32, "nl": 16, "pf": 32, "pd": 32,
-                "dl": 32, "t1": 32, "t2": 32, "fl": 32, "arow": K, "brow": K, "asc": K, "md": K, "hold": K, "aca": 16,
-                "acb": 16, "rka": 16, "rkb": 16, "kl": 16, "e2": 16, "gl": 16, "esc": 16, "cc": 16, "ef": 16, "af": 16,
+                "dl": 32, "t1": 32, "t2": 32, "fl": 32, "arow": K, "brow": K, "asc": K, "md": K, "hold": 2 * K, "aca": 16,
+                "acb": 16, "rka": 16, "rkb": 16, "kl": 16, "e2": 16, "gl": 32, "esc": 16, "cc": 16, "ef": 16, "af": 16,
                 "prow": C, "yt": C},
     "int32": {"pi": 8, "pq": 8, "ptl": 28},
     "uint16": {"qo": 28, "uo": 8, "pu": 32, "lu": 64, "pe": 16, "yl": 16, "ku": 16, "ru": 16, "eu": 16, "au": 16},
@@ -227,9 +227,13 @@ def rank_program(g, core, T, topo):
         tt(V("pd", 0, w), V("t2", 0, w), V("pf", 0, w), OP.max)
         tt(V("dl", 0, w), V("il", 0, w), V("pd", 0, w), OP.subtract)
 
-    dma("s", T.ptl[:], T.ptr[:], [], [V("ptl", 0, 28)], "dptr")
+    def planes(lo, hi):
+        for b in range(4):
+            act(V("xh", C * b + lo, C * b + hi), V("xt", 4 * lo + b, 4 * hi, 4), AF.Copy, scale=0.5)
+
     dma("y", T.xt[:, 0:4 * K], T.x[:, 0:4 * K], [], [V("xt", 0, 4 * K)], "dxa")
     dma("s", T.ut[:], T.u[:], [], [V("ut", 0, 512)], "du")
+    dma("s", T.ptl[:], T.ptr[:], [], [V("ptl", 0, 28)], "dptr")
     dma("y", T.xt[:, 4 * K:4 * C], T.x[:, 4 * K:4 * C], [], [V("xt", 4 * K, 4 * C)], "dxb")
     add("g", lambda q: q.iota(T.pi[:, 0:1], [[0, 1]], 0, 1), [], [V("pi", 0, 1)])
     add("g", lambda q: q.iota(T.iot[:], [[1, RW]], 0, 0, allow_small_or_imprecise_dtypes=True), [], [V("iot", 0, RW)])
@@ -239,7 +243,7 @@ def rank_program(g, core, T, topo):
     for nm in ("ra", "rb", "rc"):
         fill(V(nm, C, RW), float(C - K))
     fill(V("asc", 0, K), 0.0)
-    fill(V("gl", 0, 16), 0.0)
+    fill(V("gl", 0, 32), 0.0)
     fill(NEG1, -1.0)
     fill(NEGK, -float(K))
     fill(NEGK1, -float(K + 1))
@@ -259,9 +263,11 @@ def rank_program(g, core, T, topo):
     ts(V("w16", 0, 16), V("w16", 0, 16), BIG, OP.add)
     ts(V("w16", 16, 32), V("w16", 16, 32), BIG, OP.subtract)
     tt(V("w16", 32, 48), V("w16", 32, 48), V("w16", 48, 64), OP.add)
+    act(V("iom", 0, RW), V("iot", 0, RW), AF.Identity, bias=NEGK)
     act(V("mk", 0, K), V("w16", 0, 16), AF.Copy, off=V("qo", 0, NK))
     act(V("rst", 0, K), V("w16", 16, 32), AF.Copy, off=V("qo", 0, NK))
     act(V("keep", 0, K), V("w16", 64, 80), AF.Copy, off=V("qo", 0, NK))
+    planes(0, K)
     quant(V("qu", 0, 128), V("su", 0, 128), V("ut", 0, 512))
     copy(V("uo", 0, 8), V("iot", 0, 128, 16))
     add("v", lambda q: q.tensor_copy(T.qr[:, 0:128].bitcast(dt.uint32), T.qu[:, 0:128].bitcast(dt.uint32).indirect(T.uo[:, 0:8])),
@@ -279,45 +285,57 @@ def rank_program(g, core, T, topo):
         for b in bs:
             quant(V("qe", 128 * b, 128 * b + 128), V("se", 128 * b, 128 * b + 128), V("et", 3 - b, 515 - b))
 
-    def planes(lo, hi):
-        for b in range(4):
-            act(V("xh", C * b + lo, C * b + hi), V("xt", 4 * lo + b, 4 * hi, 4), AF.Copy, scale=0.5)
+    HALF = [(BK_A, "arow", "fa", "aca", "rka"), (BK_B, "brow", "fb", "acb", "rkb")]
 
-    def ranks(bank, row, fn, an, rn, between=None):
-        H = K // 2
-        tt(V("md", 0, K), P(bank), V("mk", 0, K), OP.max)
-        scan(V("hold", 0, K), V("rst", 0, K), V("md", 0, K), BIG, OP.max, OP.min)
-        for k in range(NV, NK):
-            act(V(fn, K * k, K * k + K), V(row, 0, K), AF.Sign, scale=-1.0, bias=V("hold", 16 * k + 15, 16 * k + 16))
-        for k in range(NV, NK - 1):
+    def own(h, k):
+        return V("hold", K * h + 16 * k + 15, K * h + 16 * k + 16)
+
+    def own_scores(h, nv):
+        c = 16 * nv
+        for lo, hi in ((c, K), (0, c)):
+            tt(V("md", lo, hi), P(HALF[h][0], lo, hi), V("mk", lo, hi), OP.max)
+        for lo, hi in ((c, K), (0, c)):
+            scan(V("hold", K * h + lo, K * h + hi), V("rst", lo, hi), V("md", lo, hi), BIG, OP.max, OP.min)
+
+    def ranks_scalar(h, nv):
+        bank, row, fn, an, rn = HALF[h]
+        for k in range(nv, NK):
+            act(V(fn, K * k, K * k + K), V(row, 0, K), AF.Sign, scale=-1.0, bias=own(h, k))
+        for k in range(nv, NK - 1):
             c = 16 * k + 16
-            act(V(fn, K * k + c, K * k + K), V(fn, K * k + c, K * k + K), AF.Relu, scale=-1.0, acc=V("gl", k, k + 1))
-        for k in range(NV, NK):
+            act(V(fn, K * k + c, K * k + K), V(fn, K * k + c, K * k + K), AF.Relu, scale=-1.0, acc=V("gl", 16 * h + k, 16 * h + k + 1))
+        for k in range(nv, NK):
             c = 16 * k + 16
             act(V(fn, K * k, K * k + c), V(fn, K * k, K * k + c), AF.Relu, acc=V(an, k, k + 1))
 
+    def ranks_vector(h, nv, between=None):
+        bank, row, fn, an, rn = HALF[h]
+        H = K // 2
+
         def total(k):
             scan(V("sm", H * k, H * k + H), V(fn, K * k, K * k + H), V(fn, K * k + H, K * k + K), 0.0, OP.add, OP.add)
-        for k in range(NV):
-            s, c = V("hold", 16 * k + 15, 16 * k + 16), 16 * k + 16
+        for k in range(nv):
+            s, c = own(h, k), 16 * k + 16
             ts(V(fn, K * k, K * k + c), P(bank, 0, c), s, OP.is_ge)
             ts(V(fn, K * k + c, K * k + K), P(bank, c, K), s, OP.is_gt)
             if k > 0:
                 total(k - 1)
-            if k == NV - 2:
-                tt(V("eq", 0, K), P(bank), V("hold", 0, K), OP.is_equal)
+            if k == nv - 2:
+                tt(V("eq", 0, K), P(bank), V("hold", K * h, K * h + K), OP.is_equal)
             if between is not None:
                 between(k)
         scan(V("es", 0, K), V("keep", 0, K), V("eq", 0, K), 0.0, OP.mult, OP.add)
-        tt(V("esc", NV, NK), V("cc", NV, NK), V("gl", NV, NK), OP.add)
-        total(NV - 1)
-        tt(V("esc", NV, NK), V("esc", NV, NK), V("es", 16 * NV + 15, K, 16), OP.subtract)
-        tt(V(rn, 0, NV), V("sm", H - 1, H * NV, H), V("es", 15, 16 * NV, 16), OP.subtract)
-        tt(V(rn, NV, NK), V("esc", NV, NK), V(an, NV, NK), OP.subtract)
+        tt(V("esc", nv, NK), V("cc", nv, NK), V("gl", 16 * h + nv, 16 * h + NK), OP.add)
+        total(nv - 1)
+        tt(V("esc", nv, NK), V("esc", nv, NK), V("es", 16 * nv + 15, K, 16), OP.subtract)
+        tt(V(rn, 0, nv), V("sm", H - 1, H * nv, H), V("es", 15, 16 * nv, 16), OP.subtract)
+        tt(V(rn, nv, NK), V("esc", nv, NK), V(an, nv, NK), OP.subtract)
 
-    def sort_a():
+    def keys_a():
         ts(V("ku", 0, NK), V("rka", 0, NK), -1.0, OP.mult, float(K - 1), OP.add)
         ts(V("kl", 0, NK), V("rka", 0, NK), -1.0, OP.mult, float(K - 1), OP.add)
+
+    def sort_a():
         add("v", lambda q: q.tensor_copy(T.asc[:, 0:K].indirect(T.ku[:, 0:NK]), T.arow[:, 0:K]),
             [V("arow", 0, K), V("ku", 0, NK)], [V("asc", 0, K)])
 
@@ -351,9 +369,8 @@ def rank_program(g, core, T, topo):
         ts(V("fl", 0, NK), V("kl", 0, NK), nb, OP.is_ge)
         if w == C:
             ts(V("fl", NK, 2 * NK), V("rkb", 0, NK), nb, OP.is_lt)
-        ts(V("f", 0, K), V("krow", 0, K), nb, OP.is_ge)
         tt(V("t1", 0, nw), V("fl", 0, nw), V("dl", 0, nw), OP.mult)
-        scan(V("cum", 0, C), V("one", 0, C), V("f", 0, C), 0.0, OP.mult, OP.add)
+        ts(V("f", 0, K), V("krow", 0, K), nb, OP.is_ge)
         tt(V("t2", 0, nw), V("t1", 0, nw), V("pd", 0, nw), OP.add)
         L = [V("lu", 0, nw), V("lu", 32, 32 + nw)]
         rows = ["ra", "rb", "rc"]
@@ -364,10 +381,10 @@ def rank_program(g, core, T, topo):
                 total_e(range(st["total"], st["count"]))
                 st["total"] = st["count"]
             elif st["tail"] == 1:
-                copy(V("xp", 0, K), V("pr", 0, C), EU)
+                copy(EU, V("e2", 0, NK))
                 st["tail"] = 2
             elif st["tail"] == 3:
-                ts(V("pe", 0, NK), V("ms2", 15, K, 16), OFFK, OP.subtract)
+                to_list(V("xp", 0, K), "ms2")
                 st["tail"] = 4
 
         def counts(s):
@@ -375,16 +392,18 @@ def rank_program(g, core, T, topo):
             st["count"] += share[s]
             if st["total"] == NK and st["tail"] == 0:
                 tt(V("e2", 0, NK), V("sm", FW // 2 - 1, NK * FW // 2, FW // 2), V("iot", 0, K, 16), OP.add)
-                copy(EU, V("e2", 0, NK))
                 st["tail"] = 1
             elif st["tail"] == 2:
-                to_list(V("xp", 0, K), "ms2")
+                copy(V("xp", 0, K), V("pr", 0, C), EU)
                 st["tail"] = 3
+            elif st["tail"] == 4:
+                ts(V("pe", 0, NK), V("ms2", 15, K, 16), OFFK, OP.subtract)
+                st["tail"] = 5
 
-        count_e([0])
         copy(L[0], V("t2", 0, nw))
+        scan(V("cum", 0, C), V("one", 0, C), V("f", 0, C), 0.0, OP.mult, OP.add)
         both(V(rows[0], 0, w), V("iom", 0, RW), L[0], nv)
-        count_e(range(1, share[0]))
+        count_e(range(0, share[0]))
         st["count"] = share[0]
         both(V(rows[1], 0, w), V(rows[0], 0, RW), L[0], nv)
         totals()
@@ -397,7 +416,7 @@ def rank_program(g, core, T, topo):
                 totals()
                 ts(L[s % 2], lst, OFFK, OP.subtract)
                 counts(s + 1)
-        while st["tail"] < 4:
+        while st["tail"] < 5:
             totals()
             counts(len(share) - 1)
         copy(V("exb", 0, K), V(a, 0, RW), V("pe", 0, NK))
@@ -406,7 +425,7 @@ def rank_program(g, core, T, topo):
         ts(V("yl", 0, NK), lst, OFFK, OP.subtract)
         for p in range(4):
             if p == 1:
-                both(V("xr", 0, K), V(b, 0, RW), V("yl", 0, NK), NK)
+                both(V("xr", 0, K), V(b, 0, RW), V("yl", 0, NK), 8)
             act(V("vh", K * p, K * p + K), V("xh", C * p, C * p + C), AF.Copy, off=EU)
         tt(V("af", 0, NK), to_list(V("xr", 0, K)), V("ef", 0, NK), OP.min)
         ts(V("au", 0, NK), V("af", 0, NK), OFFK, OP.subtract)
@@ -445,7 +464,7 @@ def rank_program(g, core, T, topo):
         for b in range(4):
             mm(P(b), V("lqw", 128 * b, 128 * b + 128), V("lsw", 128 * b, 128 * b + 128), V("lq%d" % t, 0, K), V("ls%d" % t, 0, K))
         for b in range(4):
-            if b % 2 == 0:
+            if b % 2 == 0 or gap is not None:
                 act(V("ht", b, 4 * K, 4), P(b), AF.Relu, scale=0.03125)
             else:
                 ts(V("ht", b, 4 * K, 4), P(b), 0.0, OP.max, 0.03125, OP.mult)
@@ -455,7 +474,7 @@ def rank_program(g, core, T, topo):
         for b in range(4):
             mm(P(b), V("qe", 128 * b, 128 * b + 128), V("se", 128 * b, 128 * b + 128), V("qh", 0, K), V("sh", 0, K))
         for b in range(4):
-            if b % 2 == 0:
+            if b % 2 == 0 or gap is not None:
                 act(V("xt", 4 * K + b, 4 * C, 4), P(b), AF.Copy)
             else:
                 copy(V("xt", 4 * K + b, 4 * C, 4), P(b))
@@ -471,20 +490,25 @@ def rank_program(g, core, T, topo):
     act(V("arow", 0, K), P(BK_A2), AF.Copy)
 
     def second_half(k):
-        if k == 3:
+        if k == 1:
             quant(QB[0], QB[1], V("xt", 4 * K, 4 * C))
             mm(P(BK_B), UR[0], UR[1], QB[0], QB[1])
             mm(P(BK_B2), UR[0], UR[1], QB[0], QB[1])
+        if k == 4:
+            own_scores(1, NV["b0"])
+            act(V("brow", 0, K), P(BK_B2), AF.Copy)
+            ranks_scalar(1, NV["b0"])
 
-    ranks(BK_A, "arow", "fa", "aca", "rka", second_half)
-    act(V("brow", 0, K), P(BK_B2), AF.Copy)
+    own_scores(0, NV["a0"])
+    ranks_scalar(0, NV["a0"])
+    ranks_vector(0, NV["a0"], second_half)
+    keys_a()
+    later_constants()
     sort_a()
-    act(V("iom", 0, RW), V("iot", 0, RW), AF.Identity, bias=NEGK)
+    ranks_vector(1, NV["b0"])
     rank_row()
-    act(V("cap", 0, C), V("w16", 32, 48), AF.Copy, off=V("qo", 0, 28))
-    ranks(BK_B, "brow", "fb", "acb", "rkb", lambda k: later_constants() if k == NV - 1 else None)
     act(V("pr", 0, C), V("iom", 0, RW), AF.Copy, off=V("pu", 0, 28))
-    planes(0, K)
+    act(V("cap", 0, C), V("w16", 32, 48), AF.Copy, off=V("qo", 0, 28))
     planes(K, C)
     for t in range(R):
         select()
@@ -497,23 +521,28 @@ def rank_program(g, core, T, topo):
             act(V("arow", 0, K), P(BK_A2), AF.Copy)
             if t == 0:
                 unit_tiles([0, 1])
-            ranks(BK_A, "arow", "fa", "aca", "rka")
-            planes(0, K)
+            own_scores(0, NV["a"])
+            ranks_scalar(0, NV["a"])
+            ranks_vector(0, NV["a"])
             if t == 0:
                 unit_tiles([2, 3])
-            sort_a()
+            keys_a()
 
             def gap():
-                rank_row()
+                planes(0, K)
+                sort_a()
                 ts(V("pf", 0, NK), to_list(V("pr", 0, K)), OFFK, OP.subtract)
                 if t == 0:
                     copy(V("pr", K, C), V("iom", 0, K))
             arrive(t, gap)
             mm(P(BK_B), UR[0], UR[1], QB[0], QB[1])
             mm(P(BK_B2), UR[0], UR[1], QB[0], QB[1])
+            rank_row()
             pointer_lists(NK)
             act(V("brow", 0, K), P(BK_B2), AF.Copy)
-            ranks(BK_B, "brow", "fb", "acb", "rkb")
+            own_scores(1, NV["b"])
+            ranks_scalar(1, NV["b"])
+            ranks_vector(1, NV["b"])
             planes(K, C)
         else:
             mm(P(BK_A), V("qu", 0, 128), V("su", 0, 128), QA[0], QA[1])

@@ -1,30 +1,39 @@
+import numpy as np
 from concourse.bass import DstId, RemoteDMATransfer
-from concourse.mybir import dt, AluOpType, ActivationFunctionType
+from concourse.mybir import dt, AluOpType, AxisListType, ActivationFunctionType
 
 C, K, R, NK = 448, 224, 3, 14
-FW = K + 16
+Z = 16
 RW = C + 16
+W2 = K + 16
 BIG = 1e29
 LIFT = 1024.0
-NV = {"a0": 8, "b0": 6, "a": 8, "b": 8}
+RBASE = 49152.0
+NV = {"a0": 9, "b0": 9, "a": 9, "b": 9}
 STEPS = 9
-SPLIT = {C: 4, K: 0}
-SHARE = {C: [3, 2, 2, 2, 2, 2, 1, 0, 0, 0, 0], K: [3, 2, 2, 2, 2, 2, 1, 0, 0, 0, 0]}
+JUMP = 32
+SPLIT, CLV, SQV, XPV, XBV, XV = [10] * 11, [4] * 6, 0, 0, 6, 8
+RR2 = [False, True]
+EVAC, EVAC2 = "svsv", "svsv"
+TRAVEL = 3.3
 CODE = "float8_e4m3fn_x4"
 
 BUFFERS = {
-    "bfloat16": {"xt": 4 * C, "xh": 4 * C, "ut": 512, "ht": 4 * K, "vh": 4 * K, "et": 520, "one": 520, "iom": RW,
-                 "cap": C, "keep": K, "fa": NK * K, "fb": NK * K, "junk": NK * FW, "eq": K, "es": K, "krow": K, "f": C,
-                 "cb": K, "cum": C, "ra": RW, "rb": RW, "rc": RW, "pr": C, "exb": K, "xr": K, "xp": K, "sm": NK * FW // 2},
-    "float16": {"ms": C, "ms2": K},
-    "float32": {"iot": RW, "w16": 80, "off": 8, "qf": 8, "mk": K, "rst": K, "il": 32, "nl": 16, "pf": 32, "pd": 32,
-                "dl": 32, "t1": 32, "t2": 32, "fl": 32, "arow": K, "brow": K, "asc": K, "md": K, "hold": 2 * K, "aca": 16,
-                "acb": 16, "rka": 16, "rkb": 16, "kl": 16, "e2": 16, "gl": 32, "esc": 16, "cc": 16, "ef": 16, "af": 16,
-                "prow": C, "yt": C},
+    "bfloat16": {"xt": 4 * C, "xh": 4 * C, "ut": 512, "ht": 4 * K, "vh": 4 * K, "et": 520, "one": 520, "iom": RW, "kk": K,
+                 "cap": C, "keep": K, "fv": 2 * NK * K, "eq": 2 * K, "es": 2 * K, "krow": K, "fb": K, "ta": K, "tb": K,
+                 "cb": K, "cum": RW, "ra": RW, "rb": RW, "rc": RW, "rd": RW, "pr": C, "exb": K, "rr": C, "gw": C,
+                 "pw": 2 * RW, "pa": 2 * RW, "pb": 2 * RW, "ca": 2 * RW, "cc": 2 * RW, "da": 2 * RW, "db": 2 * RW,
+                 "fp": 2 * K, "cp": K, "junk": C, "xr": K, "xp": K, "sm": NK * K},
+    "float16": {"ms": 4 * C, "mx": 2 * K},
+    "float32": {"iot": RW, "w16": 80, "i16": 48, "off": 16, "qf": 8, "mk": K, "rst": K, "il": 32, "pf": 32, "t1": 32, "t2": 32,
+                "t3": 32, "t4": 32, "pd": 32, "dl": 32, "fl": 32, "kl": 32, "sc": 8, "j16": 32, "p16": 32,
+                "arow": K, "brow": K, "asc": K, "md": 2 * K, "hold": 2 * K, "an": 32, "fs": 2 * NK * W2, "ce": 16, "er": 16,
+                "ne": 16, "ea": 8, "ef": 16, "af": 16, "sr4": C, "prow": C, "yt": C},
     "int32": {"pi": 8, "pq": 8, "ptl": 28},
-    "uint16": {"qo": 28, "uo": 8, "pu": 32, "lu": 64, "pe": 16, "yl": 16, "ku": 16, "ru": 16, "eu": 16, "au": 16},
-    CODE: {"qx": C, "qu": 128, "qr": 128, "qw": 512, "qe": 512, "qh": K},
-    "uint8": {"sx": C, "su": 128, "sr": 128, "sw": 512, "se": 512, "sh": K},
+    "uint16": {"qo": 28, "uo": 8, "lu": 128, "lp": 128, "pu": 32, "pe": 16, "yl": 16, "ku": 16, "ru": 16, "eu": 16, "au": 16,
+               "nu": 16, "bu": 8, "gu": 8},
+    CODE: {"qx": (R + 1) * C, "qu": 128, "qr": 128, "qw": 512, "qe": 512, "qh": K},
+    "uint8": {"sx": (R + 1) * C, "su": 128, "sr": 128, "sw": 512, "se": 512, "sh": K},
 }
 STAGES = [("w", 512)] + [(str(_t), K) for _t in range(R)]
 for _t, _w in STAGES:
@@ -32,13 +41,18 @@ for _t, _w in STAGES:
     BUFFERS["uint8"].update({"rs" + _t: _w, "ls" + _t: _w})
 SCRATCH = {_n: ("sbuf", [128, _w], _d) for _d in BUFFERS for _n, _w in BUFFERS[_d].items()}
 SCRATCH["ps"] = ("psum", [128, 4096], "float32")
+WIDE = {_n: (2 if _d in ("bfloat16", "float16", "uint16") else 4) for _d in BUFFERS for _n in BUFFERS[_d]}
+WIDE["ps"] = 4
 
 SEMAPHORES = ["cv", "cs", "cp", "cg", "dptr", "du", "dxa", "dxb", "dwc", "dws", "st", "sent"] + \
     [_n + _t for _t, _w in STAGES for _n in ("out", "hop", "arr")]
 
 OP = AluOpType
 AF = ActivationFunctionType
-BK_A, BK_A2, BK_B, BK_B2 = 4, 5, 6, 7
+BK_A, BK_A2, BK_B, BK_B2 = 7, 6, 5, 4
+CYC, LAT, LATX, GAT, SCA, TTG, PSX, PFX, PEC, VFX, SFX = 0.00086, 0.2, 0.15, 1.45, 3.0, 0.7, 0.01, 0.04, 0.00083, 0.005, 0.03
+SEED, TRIALS, SHAKE = 0, 150, 0.3
+PLAN = {}
 
 
 def relays(src, dst, topo):
@@ -85,9 +99,73 @@ def clash(a, b):
     return not (a[3] > 1 and a[3] == b[3] and (a[1] - b[1]) % a[3] != 0)
 
 
-def emit(g, T, ops):
-    eng = {"v": g.vector, "s": g.scalar, "p": g.tensor, "g": g, "y": g.sync}
-    csem = {"v": "cv", "s": "cs", "p": "cp", "g": "cg"}
+def ordered(o, e):
+    return any(clash(a, b) for a in o["r"] for b in e["w"]) or any(clash(a, b) for a in o["w"] for b in e["w"] + e["r"]) or \
+        (e["q"] != o["q"] and any(a[0] == "ps" and clash(a, b) for a in o["r"] for b in e["r"]))
+
+
+def place(seq, pre, dur, queue):
+    busy = {}
+    start = [0.0] * len(dur)
+    for i in seq:
+        t = 0.0
+        for j, lag in pre[i]:
+            t = max(t, start[j] + dur[j] + lag)
+        line = busy.setdefault(queue[i], [])
+        k = 0
+        while k < len(line) and line[k][0] < t + dur[i] - 1e-9:
+            t = max(t, line[k][1])
+            k += 1
+        line.insert(k, (t, t + dur[i]))
+        start[i] = t
+    return start
+
+
+def arrange(ops):
+    n = len(ops)
+    by = {}
+    pre, post = [], [[] for _ in range(n + 1)]
+    for i, o in enumerate(ops):
+        names = set(v[0] for v in o["r"] + o["w"])
+        cand = set(j for nm in names for j in by.get(nm, []))
+        p = {j: (LAT if ops[j]["q"] == o["q"] else LATX) + ops[j]["d"] - ops[j]["occ"] for j in cand if ordered(o, ops[j])}
+        for j, lag in o["after"]:
+            p[j] = max(p.get(j, lag), lag)
+        pre.append(sorted(p.items()))
+        for nm in names:
+            by.setdefault(nm, []).append(i)
+    pre.append([(j, ops[j]["d"] - ops[j]["occ"]) for j in range(n)])
+    for i in range(n + 1):
+        for j, lag in pre[i]:
+            post[j].append((i, lag))
+    dur = [o["occ"] for o in ops] + [0.0]
+    queue = [o["q"] for o in ops] + ["end"]
+    up = [0.0] * (n + 1)
+    for i in range(n, -1, -1):
+        up[i] += dur[i]
+        for j, lag in pre[i]:
+            up[j] = max(up[j], up[i] + lag)
+    rng = np.random.default_rng(SEED)
+    best = None
+    for trial in range(TRIALS):
+        key = list(up)
+        if trial:
+            noise = rng.random(n + 1) * SHAKE
+            key = [0.0] * (n + 1)
+            base = up if trial % 4 == 1 else [-x for x in best[1]]
+            for i in range(n, -1, -1):
+                key[i] = max([base[i] + float(noise[i])] + [key[j] + 1e-6 for j, lag in post[i]])
+        start = place(sorted(range(n + 1), key=lambda i: (-key[i], i)), pre, dur, queue)
+        for turn in range(2):
+            back = place(sorted(range(n + 1), key=lambda i: (-start[i] - dur[i], -i)), post, dur, queue)
+            start = place(sorted(range(n + 1), key=lambda i: (-back[i] - dur[i], i)), pre, dur, queue)
+        if best is None or start[n] < best[0] + 1e-9:
+            best = (start[n], start)
+    PLAN["span"] = best[0]
+    return sorted(range(n), key=lambda i: (best[1][i], i))
+
+
+def waits(ops):
     deps = []
     for i, o in enumerate(ops):
         last = {}
@@ -96,12 +174,10 @@ def emit(g, T, ops):
             key = e["sem"] or e["q"]
             if key in last or e["quiet"]:
                 continue
-            if any(clash(a, b) for a in o["r"] for b in e["w"]) or any(clash(a, b) for a in o["w"] for b in e["w"] + e["r"]) or \
-                    (e["q"] != o["q"] and any(a[0] == "ps" and clash(a, b) for a in o["r"] for b in e["r"])):
+            if ordered(o, e):
                 last[key] = j
         deps.append(sorted(last.values()))
-    need = set()
-    known = {q: {} for q in eng}
+    known = {q: {} for q in "vspgy"}
     clock = {}
     keep = []
     for i, o in enumerate(ops):
@@ -112,12 +188,23 @@ def emit(g, T, ops):
             if kn.get(key, -1) >= j:
                 continue
             w.append(j)
-            need.add(j)
             kn[key] = j
             for k2, v2 in clock[j].items():
                 kn[k2] = max(kn.get(k2, -1), v2)
         keep.append(w)
         clock[i] = dict(kn)
+    return keep
+
+
+def emit(g, T, ops):
+    eng = {"v": g.vector, "s": g.scalar, "p": g.tensor, "g": g, "y": g.sync}
+    csem = {"v": "cv", "s": "cs", "p": "cp", "g": "cg"}
+    if "order" not in PLAN:
+        PLAN["order"] = arrange(ops)
+        PLAN["keep"] = waits([ops[i] for i in PLAN["order"]])
+    ops = [ops[i] for i in PLAN["order"]]
+    keep = PLAN["keep"]
+    need = set(j for w in keep for j in w)
     count, total, waited = {}, {}, {}
     for i, o in enumerate(ops):
         q = eng[o["q"]]
@@ -163,30 +250,47 @@ def rank_program(g, core, T, topo):
     def tr(v):
         return ("ps", v[1] // 512 * 512, v[1] // 512 * 512 + 512, 1) if v[0] == "ps" else v
 
-    def add(q, f, r, w, sem=None, quiet=False):
-        ops.append({"q": q, "f": f, "r": [tr(v) for v in r if isinstance(v, tuple)], "w": [tr(v) for v in w],
-                    "sem": sem, "quiet": quiet})
+    def size(v):
+        return len(range(v[1], v[2], v[3]))
+
+    def add(q, f, r, w, d, sem=None, quiet=False, occ=None, after=()):
+        ops.append({"q": q, "f": f, "r": [tr(v) for v in r if isinstance(v, tuple)], "w": [tr(v) for v in w], "d": d,
+                    "occ": d if occ is None else occ, "sem": sem, "quiet": quiet, "after": list(after)})
+        return len(ops) - 1
 
     def src(v, off):
         return ap(v) if off is None else ap(v).indirect(ap(off))
 
+    def vcost(out, off, per, *sides):
+        if off is not None:
+            return 0.05 + size(out) * (GAT + (TTG if per == 2.0 else 0.0)) * CYC
+        if per is None:
+            per = 0.5 if all(WIDE[v[0]] == 2 for v in (out,) + sides) else 1.0
+        return VFX + max(64.0, size(out) * per) * CYC + (PSX if any(v[0] == "ps" for v in sides) else 0.0)
+
     def copy(out, in_, off=None):
-        add("v", lambda q: q.tensor_copy(ap(out), src(in_, off)), [in_, off], [out])
+        add("v", lambda q: q.tensor_copy(ap(out), src(in_, off)), [in_, off], [out], vcost(out, off, None, in_))
 
     def tt(out, a, b, op, off=None):
-        add("v", lambda q: q.tensor_tensor(ap(out), src(a, off), ap(b), op), [a, b, off], [out])
+        add("v", lambda q: q.tensor_tensor(ap(out), src(a, off), ap(b), op), [a, b, off], [out],
+            vcost(out, off, 1.0 if "ps" in (a[0], b[0]) else 2.0, a, b))
 
-    def ts(out, a, s1, op0, s2=None, op1=None):
+    def ts(out, a, s1, op0, s2=None, op1=None, off=None):
+        d = vcost(out, off, None, a)
         if op1 is None:
-            add("v", lambda q: q.tensor_scalar(ap(out), ap(a), ap(s1), None, op0), [a, s1], [out])
+            add("v", lambda q: q.tensor_scalar(ap(out), src(a, off), ap(s1), None, op0), [a, s1, off], [out], d)
         else:
-            add("v", lambda q: q.tensor_scalar(ap(out), ap(a), ap(s1), ap(s2), op0, op1), [a, s1, s2], [out])
+            add("v", lambda q: q.tensor_scalar(ap(out), src(a, off), ap(s1), ap(s2), op0, op1), [a, s1, s2, off], [out], d)
 
     def scan(out, d0, d1, init, op0, op1):
-        add("v", lambda q: q.tensor_tensor_scan(ap(out), ap(d0), ap(d1), init, op0, op1), [d0, d1], [out])
+        add("v", lambda q: q.tensor_tensor_scan(ap(out), ap(d0), ap(d1), ap(init), op0, op1), [d0, d1, init], [out],
+            vcost(out, None, None, d0, d1))
+
+    def least(out, in_):
+        add("v", lambda q: q.tensor_reduce(ap(out), ap(in_), AxisListType.X, OP.min), [in_], [out], vcost(in_, None, 1.0))
 
     def fill(out, c):
-        add("v", lambda q: q.memset(ap(out), c), [], [out])
+        add("v", lambda q: q.memset(ap(out), c), [], [out], vcost(out, None, None))
 
     def act(out, in_, func, off=None, scale=None, bias=None, acc=None):
         kw = {}
@@ -196,56 +300,89 @@ def rank_program(g, core, T, topo):
             kw["bias"] = ap(bias)
         if acc is not None:
             kw["accum_out"] = ap(acc)
+        d = (0.065 + size(out) * GAT * CYC if off is not None else SFX + size(out) * CYC + (PSX if in_[0] == "ps" else 0.0)) \
+            + (0.02 if acc else 0.0)
         add("s", lambda q: q.activation(ap(out), src(in_, off), func, **kw), [in_, off, bias],
-            [out] + ([acc] if acc is not None else []))
+            [out] + ([acc] if acc is not None else []), d)
 
     def quant(c, s, in_):
-        add("v", lambda q: q.quantize_mx(ap(c), ap(s), ap(in_)), [in_], [c, s])
+        add("v", lambda q: q.quantize_mx(ap(c), ap(s), ap(in_)), [in_], [c, s], 0.014 + 0.00023 * size(in_))
 
-    def mm(out, wc, ws, xc, xs):
-        add("p", lambda q: q.matmul_mx(ap(out), ap(wc), ap(ws), ap(xc), ap(xs), True, True), [wc, ws, xc, xs], [out])
+    def mm(out, wc, ws, xc, xs, first=(), after=()):
+        def f(q):
+            for sem, val in first:
+                q.wait_ge(T.sem[sem], val)
+            return q.matmul_mx(ap(out), ap(wc), ap(ws), ap(xc), ap(xs), True, True)
+        return add("p", f, [wc, ws, xc, xs], [out], (size(xc) + 16) * PEC + PFX, after=after)
 
-    def dma(qn, out, in_, r, w, sem):
-        add(qn, lambda q: q.dma_start(out, in_), r, w, sem)
+    def dma(qn, out, in_, r, w, sem, d=2.5, first=(), after=()):
+        def f(q):
+            for s, val in first:
+                q.wait_ge(T.sem[s], val)
+            return q.dma_start(out, in_)
+        return add(qn, f, r, w, d, sem, occ=0.05, after=after)
 
-    def wait(qn, sem, val):
-        add(qn, lambda q: q.wait_ge(T.sem[sem], val), [], [], quiet=True)
+    turn = [0]
 
-    def to_list(row, ms="ms"):
-        w = row[2] - row[1]
-        scan(V(ms, 0, w), V("cap", 0, w), row, 0.0, OP.add, OP.max)
-        return V(ms, 15, w, 16)
+    def to_list(row, ms=None):
+        w = size(row)
+        if ms is None:
+            ms = ("ms", C * (turn[0] % 4))
+            turn[0] += 1
+        scan(V(ms[0], ms[1], ms[1] + w), V("cap", 0, w), row, 0.0, OP.add, OP.max)
+        return V(ms[0], ms[1] + 15, ms[1] + w, 16)
 
-    OFF, OFFK, NEG1, NEGK, NEGK1 = V("off", 0, 1), V("off", 3, 4), V("off", 4, 5), V("off", 5, 6), V("off", 6, 7)
+    OFF, OFFK, NEG1, NEGK1 = V("off", 0, 1), V("off", 1, 2), V("off", 2, 3), V("off", 4, 5)
+    BQ, TE, OFFS, POSK, KEY1 = V("off", 6, 7), V("off", 7, 8), V("off", 8, 9), V("off", 9, 10), V("off", 10, 11)
     UR = (V("qr", 0, 128), V("sr", 0, 128))
-    QA = (V("qx", 0, K), V("sx", 0, K))
-    QB = (V("qx", K, C), V("sx", K, C))
 
-    def pointer_lists(w):
-        tt(V("t1", 0, w), V("pf", 0, w), V("il", 0, w), OP.is_equal)
-        ts(V("t2", 0, w), V("t1", 0, w), float(C), OP.mult)
-        tt(V("pd", 0, w), V("t2", 0, w), V("pf", 0, w), OP.max)
-        tt(V("dl", 0, w), V("il", 0, w), V("pd", 0, w), OP.subtract)
+    def QA(t):
+        return V("qx", C * t, C * t + K), V("sx", C * t, C * t + K)
+
+    def QB(t):
+        return V("qx", C * t + K, C * t + C), V("sx", C * t + K, C * t + C)
 
     def planes(lo, hi):
         for b in range(4):
             act(V("xh", C * b + lo, C * b + hi), V("xt", 4 * lo + b, 4 * hi, 4), AF.Copy, scale=0.5)
 
-    dma("y", T.xt[:, 0:4 * K], T.x[:, 0:4 * K], [], [V("xt", 0, 4 * K)], "dxa")
-    dma("s", T.ut[:], T.u[:], [], [V("ut", 0, 512)], "du")
-    dma("s", T.ptl[:], T.ptr[:], [], [V("ptl", 0, 28)], "dptr")
-    dma("y", T.xt[:, 4 * K:4 * C], T.x[:, 4 * K:4 * C], [], [V("xt", 4 * K, 4 * C)], "dxb")
-    add("g", lambda q: q.iota(T.pi[:, 0:1], [[0, 1]], 0, 1), [], [V("pi", 0, 1)])
-    add("g", lambda q: q.iota(T.iot[:], [[1, RW]], 0, 0, allow_small_or_imprecise_dtypes=True), [], [V("iot", 0, RW)])
+    def both(out, win, lst, nv):
+        if nv:
+            copy(V(out[0], out[1], out[1] + 16 * nv), win, V(lst[0], lst[1], lst[1] + nv))
+        if lst[1] + nv < lst[2]:
+            act(V(out[0], out[1] + 16 * nv, out[2]), win, AF.Copy, off=V(lst[0], lst[1] + nv, lst[2]))
+
+    def odd(name, lo, hi):
+        return V(name, 2 * (Z + lo) + 1, 2 * (Z + hi), 2)
+
+    d0 = dma("s", T.ut[:], T.u[:], [], [V("ut", 0, 512)], "du", 4.4)
+    d1 = dma("y", T.xt[:, 0:4 * K], T.x[:, 0:4 * K], [], [V("xt", 0, 4 * K)], "dxa", 3.6)
+    dma("s", T.ptl[:], T.ptr[:], [], [V("ptl", 0, 28)], "dptr", 4.6, after=[(d0, 0.0)])
+    d2 = dma("y", T.xt[:, 4 * K:4 * C], T.x[:, 4 * K:4 * C], [], [V("xt", 4 * K, 4 * C)], "dxb", 5.8, after=[(d1, 0.0)])
+    d3 = dma("y", T.qw[:].bitcast(dt.uint8), T.wc[:], [], [V("qw", 0, 512)], "dwc", 7.2, after=[(d2, 0.0)])
+    dma("y", T.sw[:], T.ws[:], [], [V("sw", 0, 512)], "dws", 7.8, after=[(d3, 0.0)])
+    add("g", lambda q: q.iota(T.pi[:, 0:1], [[0, 1]], 0, 1), [], [V("pi", 0, 1)], 0.14)
+    add("g", lambda q: q.iota(T.i16[:, 0:16], [[1, 16]], 0, 0, allow_small_or_imprecise_dtypes=True), [], [V("i16", 0, 16)], 0.16)
+    add("g", lambda q: q.iota(T.i16[:, 16:44], [[16, 28]], 0, 0, allow_small_or_imprecise_dtypes=True), [], [V("i16", 16, 44)], 0.19)
+    add("g", lambda q: q.iota(T.iom[:], [[1, RW]], -K, 0, allow_small_or_imprecise_dtypes=True), [], [V("iom", 0, RW)], 1.0)
+    add("g", lambda q: q.iota(T.iot[:], [[1, RW]], 0, 0, allow_small_or_imprecise_dtypes=True), [], [V("iot", 0, RW)], 1.0)
     fill(V("one", 0, 520), 1.0)
     add("g", lambda q: q.affine_select(T.et[:, 0:516], T.one[:, 0:516], [[-1, 516]], OP.is_equal, 0.0, 3, 4),
-        [V("one", 0, 516)], [V("et", 0, 516)])
-    for nm in ("ra", "rb", "rc"):
+        [V("one", 0, 516)], [V("et", 0, 516)], 1.1)
+    for nm in ("ra", "rb", "rc", "rd"):
         fill(V(nm, C, RW), float(C - K))
+    for nm in ("pw", "pa", "pb"):
+        fill(V(nm, 0, 2 * (Z + K)), -float(K + Z))
+    for nm in ("ca", "cc"):
+        fill(V(nm, 0, 2 * Z), -LIFT)
+    fill(V("ca", 2 * Z, 2 * (Z + K)), 1.0)
+    for nm in ("da", "db"):
+        fill(V(nm, 2 * Z, 2 * (Z + K)), 0.0)
+    fill(V("cum", C, RW), -LIFT * (Z - 1))
+    fill(POSK, float(K))
+    fill(V("kk", 0, K), LIFT)
     fill(V("asc", 0, K), 0.0)
-    fill(V("gl", 0, 32), 0.0)
     fill(NEG1, -1.0)
-    fill(NEGK, -float(K))
     fill(NEGK1, -float(K + 1))
     ts(V("pq", 0, 1), V("pi", 0, 1), 15, OP.bitwise_and)
     copy(V("qf", 0, 1), V("pq", 0, 1))
@@ -254,7 +391,14 @@ def rank_program(g, core, T, topo):
     ts(OFF, Q, 14.5, OP.is_lt, LIFT, OP.mult)
     ts(V("qo", 0, 28), V("one", 0, 28), Q, OP.mult)
     ts(OFFK, OFF, float(K), OP.subtract)
-    I16 = V("iot", 0, 16)
+    ts(OFFS, OFF, K + Z + 0.5, OP.subtract)
+    ts(BQ, Q, -16.0, OP.mult, RBASE + 120.0, OP.add)
+    ts(V("qf", 2, 3), Q, NK - 1.0, OP.min, 16.0, OP.mult)
+    ts(TE, V("qf", 2, 3), 15.5, OP.add, -LIFT, OP.mult)
+    ts(V("qf", 3, 4), Q, NK - 1.5, OP.is_gt, LIFT, OP.mult)
+    ts(V("qf", 4, 5), Q, 16.0, OP.mult, 15.0, OP.add)
+    tt(KEY1, V("qf", 3, 4), V("qf", 4, 5), OP.add)
+    I16 = V("i16", 0, 16)
     ts(V("w16", 0, 16), I16, Q, OP.is_equal, -2 * BIG, OP.mult)
     ts(V("w16", 16, 32), I16, 0.5, OP.is_lt, 2 * BIG, OP.mult)
     ts(V("w16", 32, 48), I16, Q, OP.is_equal, -2 * LIFT, OP.mult)
@@ -263,302 +407,291 @@ def rank_program(g, core, T, topo):
     ts(V("w16", 0, 16), V("w16", 0, 16), BIG, OP.add)
     ts(V("w16", 16, 32), V("w16", 16, 32), BIG, OP.subtract)
     tt(V("w16", 32, 48), V("w16", 32, 48), V("w16", 48, 64), OP.add)
-    act(V("iom", 0, RW), V("iot", 0, RW), AF.Identity, bias=NEGK)
+    ts(V("ce", 0, 16), I16, 256.0, OP.mult, RBASE + 256.0, OP.add)
     act(V("mk", 0, K), V("w16", 0, 16), AF.Copy, off=V("qo", 0, NK))
     act(V("rst", 0, K), V("w16", 16, 32), AF.Copy, off=V("qo", 0, NK))
     act(V("keep", 0, K), V("w16", 64, 80), AF.Copy, off=V("qo", 0, NK))
-    planes(0, K)
+    act(V("cap", 0, C), V("w16", 32, 48), AF.Copy, off=V("qo", 0, 28))
     quant(V("qu", 0, 128), V("su", 0, 128), V("ut", 0, 512))
-    copy(V("uo", 0, 8), V("iot", 0, 128, 16))
+    copy(V("uo", 0, 8), V("i16", 16, 24))
     add("v", lambda q: q.tensor_copy(T.qr[:, 0:128].bitcast(dt.uint32), T.qu[:, 0:128].bitcast(dt.uint32).indirect(T.uo[:, 0:8])),
-        [V("qu", 0, 128), V("uo", 0, 8)], [V("qr", 0, 128)])
-    copy(V("sr", 0, 128), V("su", 0, 128), V("uo", 0, 8))
+        [V("qu", 0, 128), V("uo", 0, 8)], [V("qr", 0, 128)], 0.22)
+    act(V("sr", 0, 128), V("su", 0, 128), AF.Copy, off=V("uo", 0, 8))
+    for b in range(4):
+        quant(V("qe", 128 * b, 128 * b + 128), V("se", 128 * b, 128 * b + 128), V("et", 3 - b, 515 - b))
 
-    def later_constants():
-        copy(V("pf", 0, 28), V("ptl", 0, 28))
-        copy(V("pu", 0, 28), V("ptl", 0, 28))
-        ts(V("il", 0, 28), V("iot", 0, C, 16), Q, OP.add)
-        ts(V("nl", 0, NK), V("iot", 0, K, 16), Q, OP.add, 0.5, OP.add)
-        pointer_lists(28)
-
-    def unit_tiles(bs):
-        for b in bs:
-            quant(V("qe", 128 * b, 128 * b + 128), V("se", 128 * b, 128 * b + 128), V("et", 3 - b, 515 - b))
-
-    HALF = [(BK_A, "arow", "fa", "aca", "rka"), (BK_B, "brow", "fb", "acb", "rkb")]
-
-    def own(h, k):
-        return V("hold", K * h + 16 * k + 15, K * h + 16 * k + 16)
-
-    def own_scores(h, nv):
+    def ranks(h, nv, bank, bank2, first):
+        row = ("arow", "brow")[h]
+        H = K // 2
+        act(V(row, 0, K), P(bank2), AF.Copy)
         c = 16 * nv
         for lo, hi in ((c, K), (0, c)):
-            tt(V("md", lo, hi), P(HALF[h][0], lo, hi), V("mk", lo, hi), OP.max)
-        for lo, hi in ((c, K), (0, c)):
-            scan(V("hold", K * h + lo, K * h + hi), V("rst", lo, hi), V("md", lo, hi), BIG, OP.max, OP.min)
+            tt(V("md", K * h + lo, K * h + hi), P(bank, lo, hi), V("mk", lo, hi), OP.max)
+            scan(V("hold", K * h + lo, K * h + hi), V("rst", lo, hi), V("md", K * h + lo, K * h + hi), BIG, OP.max, OP.min)
+        tt(V("eq", K * h, K * h + K), P(bank), V("hold", K * h, K * h + K), OP.is_equal)
+        scan(V("es", K * h, K * h + K), V("keep", 0, K), V("eq", K * h, K * h + K), 0.0, OP.mult, OP.subtract)
+        f0 = NK * W2 * h
+        ts(V("fs", f0 + W2 * nv + K + 1, f0 + W2 * NK, W2), V("es", K * h + c + 15, K * h + K, 16), -1.0, OP.mult, -16.0, OP.add)
+        for k in range(NK):
+            own, c = V("hold", K * h + 16 * k + 15, K * h + 16 * k + 16), 16 * k + 16
+            if k < nv:
+                f = NK * K * h + K * k
+                ts(V("fv", f, f + c), V(row, 0, c), own, OP.is_ge)
+                ts(V("fv", f + c, f + K), V(row, c, K), own, OP.is_gt)
+                m = NK * H * h + H * k
+                scan(V("sm", m, m + H), V("fv", f, f + H), V("fv", f + H, f + K), V("es", K * h + c - 1, K * h + c), OP.add, OP.add)
+            else:
+                f = f0 + W2 * k
+                act(V("fs", f, f + K), V(row, 0, K), AF.Sign, scale=-1.0, bias=own)
+                act(V("fs", f, f + c), V("fs", f, f + c), AF.Sign, bias=NEG1, acc=V("fs", f + K, f + K + 1))
+                act(V("fs", f + c, f + K + 2), V("fs", f + c, f + K + 2), AF.Relu, scale=-1.0, acc=V("an", 16 * h + k, 16 * h + k + 1))
+        m = NK * H * h
+        sv, ss = V("sm", m + H - 1, m + H * nv, H), V("an", 16 * h + nv, 16 * h + NK)
+        if h == 0:
+            ts(V("ku", 0, nv), sv, -1.0, OP.mult, K - 1.0, OP.add)
+            ts(V("ku", nv, NK), ss, -1.0, OP.mult, K + 15.0, OP.add)
+            add("v", lambda q: q.tensor_copy(T.asc[:, 0:K].indirect(T.ku[:, 0:NK]), T.arow[:, 0:K]),
+                [V("arow", 0, K), V("ku", 0, NK)], [V("asc", 0, K)], 0.05 + K * SCA * CYC)
+            act(V("krow", 0, K), V("iot", 0, K), AF.Copy, off=V("ku", 0, NK))
+            if first:
+                copy(V("kl", 0, NK), V("ku", 0, NK))
+            else:
+                tt(V("p16", 0, NK), V("asc", 15, K, 16), V("w16", 0, NK), OP.max)
+                least(V("sc", 0, 1), V("p16", 0, NK))
+        else:
+            copy(V("ru", 0, nv), sv)
+            ts(V("ru", nv, NK), ss, -16.0, OP.add)
+            if first:
+                copy(V("kl", NK, 2 * NK), V("ru", 0, NK))
 
-    def ranks_scalar(h, nv):
-        bank, row, fn, an, rn = HALF[h]
-        for k in range(nv, NK):
-            act(V(fn, K * k, K * k + K), V(row, 0, K), AF.Sign, scale=-1.0, bias=own(h, k))
-        for k in range(nv, NK - 1):
-            c = 16 * k + 16
-            act(V(fn, K * k + c, K * k + K), V(fn, K * k + c, K * k + K), AF.Relu, scale=-1.0, acc=V("gl", 16 * h + k, 16 * h + k + 1))
-        for k in range(nv, NK):
-            c = 16 * k + 16
-            act(V(fn, K * k, K * k + c), V(fn, K * k, K * k + c), AF.Relu, acc=V(an, k, k + 1))
+    EU, AU, NB = V("eu", 0, NK), V("au", 0, NK), V("sc", 4, 5)
 
-    def ranks_vector(h, nv, between=None):
-        bank, row, fn, an, rn = HALF[h]
-        H = K // 2
+    def LST(s, lo=0, hi=NK):
+        return V("lp", 16 * s + lo, 16 * s + hi)
 
-        def total(k):
-            scan(V("sm", H * k, H * k + H), V(fn, K * k, K * k + H), V(fn, K * k + H, K * k + K), 0.0, OP.add, OP.add)
-        for k in range(nv):
-            s, c = own(h, k), 16 * k + 16
-            ts(V(fn, K * k, K * k + c), P(bank, 0, c), s, OP.is_ge)
-            ts(V(fn, K * k + c, K * k + K), P(bank, c, K), s, OP.is_gt)
-            if k > 0:
-                total(k - 1)
-            if k == nv - 2:
-                tt(V("eq", 0, K), P(bank), V("hold", K * h, K * h + K), OP.is_equal)
-            if between is not None:
-                between(k)
-        scan(V("es", 0, K), V("keep", 0, K), V("eq", 0, K), 0.0, OP.mult, OP.add)
-        tt(V("esc", nv, NK), V("cc", nv, NK), V("gl", 16 * h + nv, 16 * h + NK), OP.add)
-        total(nv - 1)
-        tt(V("esc", nv, NK), V("esc", nv, NK), V("es", 16 * nv + 15, K, 16), OP.subtract)
-        tt(V(rn, 0, nv), V("sm", H - 1, H * nv, H), V("es", 15, 16 * nv, 16), OP.subtract)
-        tt(V(rn, nv, NK), V("esc", nv, NK), V(an, nv, NK), OP.subtract)
+    def spaced(out, lst):
+        ts(out, lst, OFFS, OP.subtract, 2.0, OP.mult)
 
-    def keys_a():
-        ts(V("ku", 0, NK), V("rka", 0, NK), -1.0, OP.mult, float(K - 1), OP.add)
-        ts(V("kl", 0, NK), V("rka", 0, NK), -1.0, OP.mult, float(K - 1), OP.add)
+    def gather2(name, win, s, nv, lo=0):
+        mid = max(lo, 16 * nv)
+        if mid > lo:
+            copy(odd(name, lo, mid), win, LST(s, lo // 16, nv))
+        if mid < K:
+            act(odd(name, mid, K), win, AF.Copy, off=LST(s, mid // 16, NK))
 
-    def sort_a():
-        add("v", lambda q: q.tensor_copy(T.asc[:, 0:K].indirect(T.ku[:, 0:NK]), T.arow[:, 0:K]),
-            [V("arow", 0, K), V("ku", 0, NK)], [V("asc", 0, K)])
+    def powers(lst, off):
+        ts(V("nu", 0, NK), lst, off, OP.subtract, float(C), OP.min)
+        act(odd("pw", 0, K), V("cum", 0, RW), AF.Identity, off=V("nu", 0, NK), scale=1.0 / LIFT, bias=NEGK1)
+        spaced(LST(0), to_list(odd("pw", 0, K)))
+        a, s = "pw", 0
+        while 2 ** s < JUMP:
+            b = "pa" if s % 2 == 0 else "pb"
+            lo = JUMP if 2 ** (s + 1) == JUMP else 0
+            gather2(b, V(a, 0, 2 * (Z + K)), s, SQV, lo)
+            spaced(LST(s + 1, lo // 16, NK), to_list(odd(b, lo, K)))
+            a, s = b, s + 1
 
-    def rank_row():
-        act(V("krow", 0, K), V("iot", 0, K), AF.Copy, off=V("ku", 0, NK))
+    def numbers(off):
+        tt(V("er", 0, 16), V("iot", 0, C), V("ce", 0, 16), OP.add, off=V("bu", 0, 1))
+        tt(V("ne", 0, 16), V("sr4", 0, C), V("er", 0, 16), OP.subtract, off=V("bu", 0, 1))
+        ts(EU, V("ne", 0, NK), -1.0, OP.mult)
+        ts(V("ef", 0, NK), V("ne", 0, NK), -1.0, OP.mult, off, OP.add)
+        for b in range(4):
+            act(V("vh", K * b, K * b + K), V("xh", C * b, C * b + C), AF.Copy, off=EU)
 
-    def count_e(ks):
-        for k in ks:
-            ts(V("junk", FW * k, FW * k + FW), V("cum", 16 * k, 16 * k + FW), V("nl", k, k + 1), OP.is_lt)
+    def way(h):
+        scan(V("sr4", K * h, K * h + K), V("one", 0, K), V("rr", K * h, K * h + K), V("sr4", K - 1, K) if h else 0.0, OP.add, OP.max)
 
-    def total_e(ks):
-        h = FW // 2
-        for k in ks:
-            scan(V("sm", h * k, h * k + h), V("junk", FW * k, FW * k + h), V("junk", FW * k + h, FW * k + FW), 0.0, OP.add, OP.add)
+    def ancestors(t, off):
+        lst = to_list(V("xr", 0, K), ("mx", K))
+        tt(V("af", 0, NK), lst, V("ef", 0, NK), OP.min)
+        ts(AU, V("af", 0, NK), off, OP.subtract)
+        if t < R - 1:
+            powers(lst, off)
 
-    def select():
-        copy(V("ru", 0, NK), V("rkb", 0, NK))
-        tt(V("f", K, C), V("asc", 0, K), V("brow", 0, K), OP.is_lt, off=V("ru", 0, NK))
-        scan(V("cb", 0, K), V("one", 0, K), V("f", K, C), 0.0, OP.mult, OP.add)
-
-    def both(out, win, lst, nv):
-        if nv:
-            copy(V(out[0], out[1], out[1] + 16 * nv), win, V(lst[0], lst[1], lst[1] + nv))
-        if lst[1] + nv < lst[2]:
-            act(V(out[0], out[1] + 16 * nv, out[2]), win, AF.Copy, off=V(lst[0], lst[1] + nv, lst[2]))
-
-    def climb(w):
-        nw, share, nv = w // 16, SHARE[w], SPLIT[w]
-        nb = V("cb", K - 1, K)
-        EU = V("eu", 0, NK)
+    def first_round():
+        nb, nw = V("cb", K - 1, K), C // 16
+        tt(V("fb", 0, K), V("asc", 0, K), V("brow", 0, K), OP.is_lt, off=V("ru", 0, NK))
+        scan(V("cb", 0, K), V("one", 0, K), V("fb", 0, K), 0.0, OP.mult, OP.add)
         ts(V("fl", 0, NK), V("kl", 0, NK), nb, OP.is_ge)
-        if w == C:
-            ts(V("fl", NK, 2 * NK), V("rkb", 0, NK), nb, OP.is_lt)
-        tt(V("t1", 0, nw), V("fl", 0, nw), V("dl", 0, nw), OP.mult)
-        ts(V("f", 0, K), V("krow", 0, K), nb, OP.is_ge)
-        tt(V("t2", 0, nw), V("t1", 0, nw), V("pd", 0, nw), OP.add)
-        L = [V("lu", 0, nw), V("lu", 32, 32 + nw)]
-        rows = ["ra", "rb", "rc"]
-        st = {"count": 0, "total": 0, "tail": 0}
+        ts(V("fl", NK, 2 * NK), V("kl", NK, 2 * NK), nb, OP.is_lt)
+        tt(V("t3", 0, nw), V("fl", 0, nw), V("dl", 0, nw), OP.mult)
+        tt(V("t4", 0, nw), V("t3", 0, nw), V("pd", 0, nw), OP.add)
+        ts(V("ta", 0, K), V("krow", 0, K), nb, OP.is_lt, -LIFT, OP.mult)
+        scan(V("cum", 0, K), V("kk", 0, K), V("ta", 0, K), 0.0, OP.add, OP.add)
+        ts(V("cum", K, C), V("cb", 0, K), LIFT, OP.mult, V("cum", K - 1, K), OP.add)
+        ts(V("rr", 0, C), V("cum", 0, C), 16.0 / LIFT, OP.mult, BQ, OP.add)
+        act(V("junk", 0, C), V("cum", 0, C), AF.Sign, bias=TE, acc=V("ea", 0, 1))
+        ts(V("bu", 0, 1), V("ea", 0, 1), -0.5, OP.mult, C / 2.0, OP.add)
+        way(0)
+        way(1)
+        numbers(OFFK)
+        both(V("xp", 0, K), V("pr", 0, C), EU, XPV)
+        ts(V("pe", 0, NK), to_list(V("xp", 0, K), ("mx", 0)), OFFK, OP.subtract)
 
-        def totals():
-            if st["total"] < st["count"]:
-                total_e(range(st["total"], st["count"]))
-                st["total"] = st["count"]
-            elif st["tail"] == 1:
-                copy(EU, V("e2", 0, NK))
-                st["tail"] = 2
-            elif st["tail"] == 3:
-                to_list(V("xp", 0, K), "ms2")
-                st["tail"] = 4
-
-        def counts(s):
-            count_e(range(st["count"], st["count"] + share[s]))
-            st["count"] += share[s]
-            if st["total"] == NK and st["tail"] == 0:
-                tt(V("e2", 0, NK), V("sm", FW // 2 - 1, NK * FW // 2, FW // 2), V("iot", 0, K, 16), OP.add)
-                st["tail"] = 1
-            elif st["tail"] == 2:
-                copy(V("xp", 0, K), V("pr", 0, C), EU)
-                st["tail"] = 3
-            elif st["tail"] == 4:
-                ts(V("pe", 0, NK), V("ms2", 15, K, 16), OFFK, OP.subtract)
-                st["tail"] = 5
-
-        copy(L[0], V("t2", 0, nw))
-        scan(V("cum", 0, C), V("one", 0, C), V("f", 0, C), 0.0, OP.mult, OP.add)
-        both(V(rows[0], 0, w), V("iom", 0, RW), L[0], nv)
-        count_e(range(0, share[0]))
-        st["count"] = share[0]
-        both(V(rows[1], 0, w), V(rows[0], 0, RW), L[0], nv)
-        totals()
-        counts(1)
+        def L(s):
+            return V("lu", 32 * (s % 4), 32 * (s % 4) + nw)
+        copy(L(0), V("t4", 0, nw))
+        rows = ["ra", "rb", "rc", "rd"]
+        both(V(rows[0], 0, C), V("iom", 0, RW), L(0), SPLIT[0])
+        both(V(rows[1], 0, C), V(rows[0], 0, RW), L(0), SPLIT[1])
         for s in range(1, STEPS + 1):
-            a, b = rows[s % 3], rows[(s + 1) % 3]
-            both(V(b, 0, w), V(a, 0, RW), L[(s - 1) % 2], nv)
+            a, b = rows[s % 4], rows[(s + 1) % 4]
+            both(V(b, 0, C), V(a, 0, RW), L(s - 1), SPLIT[s + 1])
             if s < STEPS:
-                lst = to_list(V(a, 0, w))
-                totals()
-                ts(L[s % 2], lst, OFFK, OP.subtract)
-                counts(s + 1)
-        while st["tail"] < 5:
-            totals()
-            counts(len(share) - 1)
-        copy(V("exb", 0, K), V(a, 0, RW), V("pe", 0, NK))
-        lst = to_list(V("exb", 0, K))
-        ts(V("ef", 0, NK), V("e2", 0, NK), OFFK, OP.add)
-        ts(V("yl", 0, NK), lst, OFFK, OP.subtract)
-        for p in range(4):
-            if p == 1:
-                both(V("xr", 0, K), V(b, 0, RW), V("yl", 0, NK), 8)
-            act(V("vh", K * p, K * p + K), V("xh", C * p, C * p + C), AF.Copy, off=EU)
-        tt(V("af", 0, NK), to_list(V("xr", 0, K)), V("ef", 0, NK), OP.min)
-        ts(V("au", 0, NK), V("af", 0, NK), OFFK, OP.subtract)
+                ts(L(s), to_list(V(a, 0, C)), OFFK, OP.subtract)
+        both(V("exb", 0, K), V(a, 0, RW), V("pe", 0, NK), XBV)
+        ts(V("yl", 0, NK), to_list(V("exb", 0, K)), OFFK, OP.subtract)
+        both(V("xr", 0, K), V(b, 0, RW), V("yl", 0, NK), XV)
+        ancestors(0, OFFK)
+
+    def count_over(piv, bound, i):
+        H = K // 2
+        ts(V("fp", K * i, K * i + K), P(BK_B) if i == 0 else V("brow", 0, K), piv, OP.is_gt)
+        scan(V("cp", H * i, H * i + H), V("fp", K * i, K * i + H), V("fp", K * i + H, K * i + K), 0.0, OP.add, OP.add)
+        ts(V("gu", 2 * i, 2 * i + 1), V("cp", H * i + H - 1, H * i + H), bound, OP.is_gt)
+        return V("gu", 2 * i, 2 * i + 1)
+
+    def marks(h):
+        lo, hi = K * h, K * h + K
+        scan(V("cum", lo, hi), V("kk", 0, K), V(("ta", "tb")[h], 0, K), V("cum", K - 1, K) if h else 0.0, OP.add, OP.add)
+        if RR2[h]:
+            ts(V("rr", lo, hi), V("cum", lo, hi), 16.0 / LIFT, OP.mult, BQ, OP.add)
+        else:
+            act(V("rr", lo, hi), V("cum", lo, hi), AF.Identity, scale=16.0 / LIFT, bias=BQ)
+        act(V("junk", lo, hi), V("cum", lo, hi), AF.Sign, bias=TE, acc=V("ea", h, h + 1))
+        way(h)
+
+    def later_round(t):
+        act(V("j16", 0, 16), I16, AF.Copy, off=count_over(V("sc", 0, 1), KEY1, 0), acc=V("sc", 1, 2))
+        ts(V("sc", 2, 3), V("sc", 1, 2), 16.0, OP.mult, Q, OP.add)
+        ts(V("gu", 4, 5), V("sc", 1, 2), 16.0, OP.mult, Q, OP.add)
+        tt(V("p16", 16, 32), V("asc", 0, K), V("w16", 0, 16), OP.max, off=V("gu", 4, 5))
+        least(V("sc", 3, 4), V("p16", 16, 32))
+        act(V("j16", 16, 32), I16, AF.Identity, off=count_over(V("sc", 3, 4), V("sc", 2, 3), 1), bias=V("sc", 1, 2), acc=NB)
+        ts(V("ta", 0, K), V("krow", 0, K), NB, OP.is_lt, -LIFT, OP.mult)
+        scan(odd("ca", 0, K), V("iom", 0, K), V("ta", 0, K), -LIFT, OP.max, OP.add)
+        marks(0)
+        ts(V("ea", 2, 3), V("ea", 0, 1), -float(C), OP.add)
+        a, b, s = "ca", "cc", 0
+        while 2 ** s < JUMP:
+            d = ("da", "db")[s % 2]
+            gather2(d, V(a, 0, 2 * (Z + K)), s, CLV[s])
+            scan(V(b, 2 * Z, 2 * (Z + K)), V(d, 2 * Z, 2 * (Z + K)), V(a, 2 * Z, 2 * (Z + K)), 0.0, OP.mult, OP.max)
+            a, b, s = b, a, s + 1
+        for lo in range(JUMP, K, JUMP):
+            hi = min(lo + JUMP, K)
+            tt(odd(a, lo, hi), V(a, 0, 2 * (Z + lo)), odd(a, lo, hi), OP.max, off=LST(s, lo // 16, hi // 16))
+        act(V("gw", 0, K), V(a, 0, 2 * (Z + K)), AF.Abs, off=LST(0), bias=POSK)
+        act(V("gw", K, C), odd(a, 0, K), AF.Abs, bias=POSK)
+        ts(V("tb", 0, K), V("iot", 0, K), NB, OP.is_ge, -LIFT, OP.mult, off=V("ru", 0, NK))
+        marks(1)
+        ts(V("bu", 0, 1), V("ea", 1, 2), V("ea", 2, 3), OP.add, -0.5, OP.mult)
+        numbers(OFF)
+        both(V("xr", 0, K), V("gw", 0, C), EU, XV)
+        ancestors(t, OFF)
 
     rl = relays(core, nxt, topo)
     en = topo.engines(core, rl[0])
     landed = sum(len(topo.engines(c, core)) for c in relays(prv, core, topo))
 
-    def send(t, qn, sn, w):
-        h, half = w // 2, len(en) // 2
+    def send(t, qv, sv):
+        w = size(qv)
+        h, hf = w // 2, len(en) // 2
 
         def calls(q):
             trs = []
             for i in range(2):
                 rid, pid = topo.addr(rl[i], core)
-                trs.append(RemoteDMATransfer(dst_ids=[DstId(rid=rid, pnc=pid)], dma_engine_mask=mask_of(en[i * half:i * half + half]),
-                                             remote_sem=T.sem["hop" + t], src=T[qn][:, i * h:i * h + h].bitcast(dt.uint8),
+                trs.append(RemoteDMATransfer(dst_ids=[DstId(rid=rid, pnc=pid)], dma_engine_mask=mask_of(en[i * hf:i * hf + hf]),
+                                             remote_sem=T.sem["hop" + t],
+                                             src=T[qv[0]][:, qv[1] + i * h:qv[1] + i * h + h].bitcast(dt.uint8),
                                              dst=T["rq" + t][:].bitcast(dt.uint8)))
             q.remote_dma_fused(trs, local_sem=T.sem["out" + t])
             rid, pid = topo.addr(rl[2], core)
-            q.remote_dma(T["rs" + t][:], T[sn][:, 0:w], T.sem["hop" + t], T.sem["out" + t], pid, rid, mask_of(en))
-        add("g", calls, [V(qn, 0, w), V(sn, 0, w)], [], quiet=True)
+            q.remote_dma(T["rs" + t][:], ap(sv), T.sem["hop" + t], T.sem["out" + t], pid, rid, mask_of(en))
+        return add("g", calls, [qv, sv], [], 0.5, quiet=True)
 
     def blend(t):
         for b in range(4):
-            tt(V("xt", b, 4 * K, 4), V("xh", C * b, C * b + C), V("vh", K * b, K * b + K), OP.add, off=V("au", 0, NK))
-            if t > 0 and b == 0:
-                wait("v", "out%d" % (t - 1), 2 * len(en))
-        quant(QA[0], QA[1], V("xt", 0, 4 * K))
-        send(str(t), "qx", "sx", K)
+            tt(V("xt", b, 4 * K, 4), V("xh", C * b, C * b + C), V("vh", K * b, K * b + K), OP.add, off=AU)
+        quant(QA(t + 1)[0], QA(t + 1)[1], V("xt", 0, 4 * K))
+        return send(str(t), QA(t + 1)[0], QA(t + 1)[1])
 
-    def arrive(t, gap=None):
-        if t == 0:
-            wait("p", "arrw", landed)
-        wait("p", "arr%d" % t, landed)
+    def arrive(t, sent):
+        first = [("arr%d" % t, landed)] + ([("arrw", landed)] if t == 0 else [])
+        after = [(sent, TRAVEL - 0.5)]
         for b in range(4):
-            mm(P(b), V("lqw", 128 * b, 128 * b + 128), V("lsw", 128 * b, 128 * b + 128), V("lq%d" % t, 0, K), V("ls%d" % t, 0, K))
+            i = mm(P(b), V("lqw", 128 * b, 128 * b + 128), V("lsw", 128 * b, 128 * b + 128),
+                   V("lq%d" % t, 0, K), V("ls%d" % t, 0, K), first if b == 0 else (), after)
+            after = [(i, 0.0)]
         for b in range(4):
-            if b % 2 == 0 or gap is not None:
+            if EVAC[b] == "s":
                 act(V("ht", b, 4 * K, 4), P(b), AF.Relu, scale=0.03125)
             else:
                 ts(V("ht", b, 4 * K, 4), P(b), 0.0, OP.max, 0.03125, OP.mult)
         quant(V("qh", 0, K), V("sh", 0, K), V("ht", 0, 4 * K))
-        if gap is not None:
-            gap()
+        after = []
         for b in range(4):
-            mm(P(b), V("qe", 128 * b, 128 * b + 128), V("se", 128 * b, 128 * b + 128), V("qh", 0, K), V("sh", 0, K))
+            i = mm(P(b), V("qe", 128 * b, 128 * b + 128), V("se", 128 * b, 128 * b + 128), V("qh", 0, K), V("sh", 0, K), (), after)
+            after = [(i, 0.0)]
         for b in range(4):
-            if b % 2 == 0 or gap is not None:
+            if EVAC2[b] == "s":
                 act(V("xt", 4 * K + b, 4 * C, 4), P(b), AF.Copy)
             else:
                 copy(V("xt", 4 * K + b, 4 * C, 4), P(b))
-        quant(QB[0], QB[1], V("xt", 4 * K, 4 * C))
+        quant(QB(t + 1)[0], QB(t + 1)[1], V("xt", 4 * K, 4 * C))
 
-    quant(QA[0], QA[1], V("xt", 0, 4 * K))
-    mm(P(BK_A), UR[0], UR[1], QA[0], QA[1])
-    mm(P(BK_A2), UR[0], UR[1], QA[0], QA[1])
-    ts(V("cc", 0, NK), V("iot", 0, K, 16), 16.0, OP.add)
-    dma("y", T.qw[:].bitcast(dt.uint8), T.wc[:], [], [V("qw", 0, 512)], "dwc")
-    dma("y", T.sw[:], T.ws[:], [], [V("sw", 0, 512)], "dws")
-    send("w", "qw", "sw", 512)
-    act(V("arow", 0, K), P(BK_A2), AF.Copy)
+    def scores(h, q, nv, first=False):
+        banks = (BK_A, BK_A2) if h == 0 else (BK_B, BK_B2)
+        for bk in banks:
+            mm(P(bk), UR[0], UR[1], q[0], q[1])
+        ranks(h, nv, banks[0], banks[1], first)
 
-    def second_half(k):
-        if k == 1:
-            quant(QB[0], QB[1], V("xt", 4 * K, 4 * C))
-            mm(P(BK_B), UR[0], UR[1], QB[0], QB[1])
-            mm(P(BK_B2), UR[0], UR[1], QB[0], QB[1])
-        if k == 4:
-            own_scores(1, NV["b0"])
-            act(V("brow", 0, K), P(BK_B2), AF.Copy)
-            ranks_scalar(1, NV["b0"])
-
-    own_scores(0, NV["a0"])
-    ranks_scalar(0, NV["a0"])
-    ranks_vector(0, NV["a0"], second_half)
-    keys_a()
-    later_constants()
-    sort_a()
-    ranks_vector(1, NV["b0"])
-    rank_row()
+    copy(V("pf", 0, 28), V("ptl", 0, 28))
+    ts(V("il", 0, 28), V("i16", 16, 44), Q, OP.add)
+    tt(V("t1", 0, 28), V("pf", 0, 28), V("il", 0, 28), OP.is_equal)
+    ts(V("t2", 0, 28), V("t1", 0, 28), float(C), OP.mult)
+    tt(V("pd", 0, 28), V("t2", 0, 28), V("pf", 0, 28), OP.max)
+    tt(V("dl", 0, 28), V("il", 0, 28), V("pd", 0, 28), OP.subtract)
+    copy(V("pu", 0, 28), V("pd", 0, 28))
     act(V("pr", 0, C), V("iom", 0, RW), AF.Copy, off=V("pu", 0, 28))
-    act(V("cap", 0, C), V("w16", 32, 48), AF.Copy, off=V("qo", 0, 28))
-    planes(K, C)
+    quant(QA(0)[0], QA(0)[1], V("xt", 0, 4 * K))
+    scores(0, QA(0), NV["a0"], True)
+    send("w", V("qw", 0, 512), V("sw", 0, 512))
+    quant(QB(0)[0], QB(0)[1], V("xt", 4 * K, 4 * C))
+    scores(1, QB(0), NV["b0"], True)
+    planes(0, C)
     for t in range(R):
-        select()
-        climb(C if t == 0 else K)
-        blend(t)
+        if t == 0:
+            first_round()
+        else:
+            later_round(t)
+        sent = blend(t)
         if t < R - 1:
-            mm(P(BK_A), UR[0], UR[1], QA[0], QA[1])
-            mm(P(BK_A2), UR[0], UR[1], QA[0], QA[1])
-            act(V("pr", 0, K), V("cum", 0, C), AF.Identity, off=V("au", 0, NK), bias=NEGK1)
-            act(V("arow", 0, K), P(BK_A2), AF.Copy)
-            if t == 0:
-                unit_tiles([0, 1])
-            own_scores(0, NV["a"])
-            ranks_scalar(0, NV["a"])
-            ranks_vector(0, NV["a"])
-            if t == 0:
-                unit_tiles([2, 3])
-            keys_a()
-
-            def gap():
-                planes(0, K)
-                sort_a()
-                ts(V("pf", 0, NK), to_list(V("pr", 0, K)), OFFK, OP.subtract)
-                if t == 0:
-                    copy(V("pr", K, C), V("iom", 0, K))
-            arrive(t, gap)
-            mm(P(BK_B), UR[0], UR[1], QB[0], QB[1])
-            mm(P(BK_B2), UR[0], UR[1], QB[0], QB[1])
-            rank_row()
-            pointer_lists(NK)
-            act(V("brow", 0, K), P(BK_B2), AF.Copy)
-            own_scores(1, NV["b"])
-            ranks_scalar(1, NV["b"])
-            ranks_vector(1, NV["b"])
+            scores(0, QA(t + 1), NV["a"])
+            planes(0, K)
+            arrive(t, sent)
+            scores(1, QB(t + 1), NV["b"])
             planes(K, C)
         else:
-            mm(P(BK_A), V("qu", 0, 128), V("su", 0, 128), QA[0], QA[1])
-            dma("y", T.oc[:, 0:4 * K], T.qx[:, 0:K].bitcast(dt.uint8), [QA[0]], [], "st")
-            act(V("prow", 0, K), V("cum", 0, C), AF.Identity, off=V("au", 0, NK), bias=NEG1)
+            qa, qb, s0 = QA(R), QB(R), C * R
+            mm(P(BK_A), V("qu", 0, 128), V("su", 0, 128), qa[0], qa[1])
+            act(V("prow", 0, K), V("cum", 0, C), AF.Identity, off=AU, scale=1.0 / LIFT, bias=NEG1)
             copy(V("prow", K, C), V("iot", 0, K))
             copy(V("yt", 0, K), P(BK_A))
-            dma("y", T.pl[:], T.prow[0:128:16, :], [V("prow", 0, C)], [], "st")
-            dma("y", T.y[:, 0:K], T.yt[:, 0:K], [V("yt", 0, K)], [], "st")
-            arrive(t)
-            mm(P(BK_B), V("qu", 0, 128), V("su", 0, 128), QB[0], QB[1])
-            dma("y", T.oc[:, 4 * K:4 * C], T.qx[:, K:C].bitcast(dt.uint8), [QB[0]], [], "st")
+            i = dma("y", T.oc[:, 0:4 * K], ap(qa[0]).bitcast(dt.uint8), [qa[0]], [], "st", first=[("out%d" % t, 2 * len(en))],
+                    after=[(sent, 1.5)])
+            i = dma("y", T.pl[:], T.prow[0:128:16, :], [V("prow", 0, C)], [], "st", after=[(i, 0.0)])
+            i = dma("y", T.y[:, 0:K], T.yt[:, 0:K], [V("yt", 0, K)], [], "st", after=[(i, 0.0)])
+            arrive(t, sent)
+            mm(P(BK_B), V("qu", 0, 128), V("su", 0, 128), qb[0], qb[1])
+            dma("y", T.oc[:, 4 * K:4 * C], ap(qb[0]).bitcast(dt.uint8), [qb[0]], [], "st", after=[(i, 0.0)])
             for k in range(4):
-                dma("y" if k < 2 else "s", T.osc[4 * k:4 * k + 4, :], T.sx[32 * k:32 * k + 4, :], [V("sx", 0, C)], [], "st")
+                dma("y" if k < 2 else "s", T.osc[4 * k:4 * k + 4, :], T.sx[32 * k:32 * k + 4, s0:s0 + C], [V("sx", s0, s0 + C)], [], "st",
+                    after=[(i, 0.0)])
             copy(V("yt", K, C), P(BK_B))
-            dma("s", T.y[:, K:C], T.yt[:, K:C], [V("yt", K, C)], [], "st")
+            dma("s", T.y[:, K:C], T.yt[:, K:C], [V("yt", K, C)], [], "st", 3.0)
     emit(g, T, ops)
-    for t in ("w", str(R - 1)):
+    for t, w in STAGES:
         g.wait_ge(T.sem["out" + t], 2 * len(en))

import numpy as np
from concourse.bass import DstId, RemoteDMATransfer
from concourse.mybir import dt, AluOpType, AxisListType, ActivationFunctionType

C, K, R, NK = 448, 224, 3, 14
Z = 16
RW = C + 16
W2 = K + 16
BIG = 1e29
LIFT = 1024.0
RBASE = 49152.0
NV = {"a0": 9, "b0": 9, "a": 9, "b": 9}
STEPS = 9
JUMP = 32
SPLIT, CLV, SQV, XPV, XBV, XV = [10] * 11, [4] * 6, 0, 0, 6, 8
RR2 = [False, True]
EVAC, EVAC2 = "svsv", "svsv"
TRAVEL = 3.3
CODE = "float8_e4m3fn_x4"

BUFFERS = {
    "bfloat16": {"xt": 4 * C, "xh": 4 * C, "ut": 512, "ht": 4 * K, "vh": 4 * K, "et": 520, "one": 520, "iom": RW, "kk": K,
                 "cap": C, "keep": K, "fv": 2 * NK * K, "eq": 2 * K, "es": 2 * K, "krow": K, "fb": K, "ta": K, "tb": K,
                 "cb": K, "cum": RW, "ra": RW, "rb": RW, "rc": RW, "rd": RW, "pr": C, "exb": K, "rr": C, "gw": C,
                 "pw": 2 * RW, "pa": 2 * RW, "pb": 2 * RW, "ca": 2 * RW, "cc": 2 * RW, "da": 2 * RW, "db": 2 * RW,
                 "fp": 2 * K, "cp": K, "junk": C, "xr": K, "xp": K, "sm": NK * K},
    "float16": {"ms": 4 * C, "mx": 2 * K},
    "float32": {"iot": RW, "w16": 80, "i16": 48, "off": 16, "qf": 8, "mk": K, "rst": K, "il": 32, "pf": 32, "t1": 32, "t2": 32,
                "t3": 32, "t4": 32, "pd": 32, "dl": 32, "fl": 32, "kl": 32, "sc": 8, "j16": 32, "p16": 32,
                "arow": K, "brow": K, "asc": K, "md": 2 * K, "hold": 2 * K, "an": 32, "fs": 2 * NK * W2, "ce": 16, "er": 16,
                "ne": 16, "ea": 8, "ef": 16, "af": 16, "sr4": C, "prow": C, "yt": C},
    "int32": {"pi": 8, "pq": 8, "ptl": 28},
    "uint16": {"qo": 28, "uo": 8, "lu": 128, "lp": 128, "pu": 32, "pe": 16, "yl": 16, "ku": 16, "ru": 16, "eu": 16, "au": 16,
               "nu": 16, "bu": 8, "gu": 8},
    CODE: {"qx": (R + 1) * C, "qu": 128, "qr": 128, "qw": 512, "qe": 512, "qh": K},
    "uint8": {"sx": (R + 1) * C, "su": 128, "sr": 128, "sw": 512, "se": 512, "sh": K},
}
STAGES = [("w", 512)] + [(str(_t), K) for _t in range(R)]
for _t, _w in STAGES:
    BUFFERS[CODE].update({"rq" + _t: _w // 2, "lq" + _t: _w})
    BUFFERS["uint8"].update({"rs" + _t: _w, "ls" + _t: _w})
SCRATCH = {_n: ("sbuf", [128, _w], _d) for _d in BUFFERS for _n, _w in BUFFERS[_d].items()}
SCRATCH["ps"] = ("psum", [128, 4096], "float32")
WIDE = {_n: (2 if _d in ("bfloat16", "float16", "uint16") else 4) for _d in BUFFERS for _n in BUFFERS[_d]}
WIDE["ps"] = 4

SEMAPHORES = ["cv", "cs", "cp", "cg", "dptr", "du", "dxa", "dxb", "dwc", "dws", "st", "sent"] + \
    [_n + _t for _t, _w in STAGES for _n in ("out", "hop", "arr")]

OP = AluOpType
AF = ActivationFunctionType
BK_A, BK_A2, BK_B, BK_B2 = 7, 6, 5, 4
CYC, LAT, LATX, GAT, SCA, TTG, PSX, PFX, PEC, VFX, SFX = 0.00086, 0.2, 0.15, 1.45, 3.0, 0.7, 0.01, 0.04, 0.00083, 0.005, 0.03
SEED, TRIALS, SHAKE = 0, 150, 0.3
PLAN = {}


def relays(src, dst, topo):
    ok = [c for c in topo.cores_of(src) if c != src and topo.may_write(c, dst)]
    near = [c for c in ok if topo.die(c) == topo.die(src)]
    far = [c for c in ok if topo.die(c) != topo.die(src)]
    return near[0], far[0], near[1]


def mask_of(engines):
    m = 0
    for e in engines:
        m |= 1 << e
    return m


def relay_program(g, core, T, topo):
    n = len(T.cores)
    for r in range(n):
        src, dst = T.cores[r], T.cores[(r + 1) % n]
        rl = relays(src, dst, topo)
        if core not in rl:
            continue
        part = rl.index(core)
        rid, pid = topo.addr(dst, core)
        m = topo.mask(core, dst)
        ne = len(topo.engines(core, dst))
        nin = len(topo.engines(src, core))
        for t, w in STAGES:
            if part < 2:
                g.wait_ge(T.sem["hop" + t], nin // 2)
                h = w // 2
                g.remote_dma(T["lq" + t][:, part * h:part * h + h].bitcast(dt.uint8), T["rq" + t][:].bitcast(dt.uint8),
                             T.sem["arr" + t], T.sem.sent, pid, rid, m)
            else:
                g.wait_ge(T.sem["hop" + t], nin)
                g.remote_dma(T["ls" + t][:], T["rs" + t][:], T.sem["arr" + t], T.sem.sent, pid, rid, m)
        g.wait_ge(T.sem.sent, len(STAGES) * ne)


def clash(a, b):
    if a[0] != b[0] or a[1] >= b[2] or b[1] >= a[2]:
        return False
    return not (a[3] > 1 and a[3] == b[3] and (a[1] - b[1]) % a[3] != 0)


def ordered(o, e):
    return any(clash(a, b) for a in o["r"] for b in e["w"]) or any(clash(a, b) for a in o["w"] for b in e["w"] + e["r"]) or \
        (e["q"] != o["q"] and any(a[0] == "ps" and clash(a, b) for a in o["r"] for b in e["r"]))


def place(seq, pre, dur, queue):
    busy = {}
    start = [0.0] * len(dur)
    for i in seq:
        t = 0.0
        for j, lag in pre[i]:
            t = max(t, start[j] + dur[j] + lag)
        line = busy.setdefault(queue[i], [])
        k = 0
        while k < len(line) and line[k][0] < t + dur[i] - 1e-9:
            t = max(t, line[k][1])
            k += 1
        line.insert(k, (t, t + dur[i]))
        start[i] = t
    return start


def arrange(ops):
    n = len(ops)
    by = {}
    pre, post = [], [[] for _ in range(n + 1)]
    for i, o in enumerate(ops):
        names = set(v[0] for v in o["r"] + o["w"])
        cand = set(j for nm in names for j in by.get(nm, []))
        p = {j: (LAT if ops[j]["q"] == o["q"] else LATX) + ops[j]["d"] - ops[j]["occ"] for j in cand if ordered(o, ops[j])}
        for j, lag in o["after"]:
            p[j] = max(p.get(j, lag), lag)
        pre.append(sorted(p.items()))
        for nm in names:
            by.setdefault(nm, []).append(i)
    pre.append([(j, ops[j]["d"] - ops[j]["occ"]) for j in range(n)])
    for i in range(n + 1):
        for j, lag in pre[i]:
            post[j].append((i, lag))
    dur = [o["occ"] for o in ops] + [0.0]
    queue = [o["q"] for o in ops] + ["end"]
    up = [0.0] * (n + 1)
    for i in range(n, -1, -1):
        up[i] += dur[i]
        for j, lag in pre[i]:
            up[j] = max(up[j], up[i] + lag)
    rng = np.random.default_rng(SEED)
    best = None
    for trial in range(TRIALS):
        key = list(up)
        if trial:
            noise = rng.random(n + 1) * SHAKE
            key = [0.0] * (n + 1)
            base = up if trial % 4 == 1 else [-x for x in best[1]]
            for i in range(n, -1, -1):
                key[i] = max([base[i] + float(noise[i])] + [key[j] + 1e-6 for j, lag in post[i]])
        start = place(sorted(range(n + 1), key=lambda i: (-key[i], i)), pre, dur, queue)
        for turn in range(2):
            back = place(sorted(range(n + 1), key=lambda i: (-start[i] - dur[i], -i)), post, dur, queue)
            start = place(sorted(range(n + 1), key=lambda i: (-back[i] - dur[i], i)), pre, dur, queue)
        if best is None or start[n] < best[0] + 1e-9:
            best = (start[n], start)
    PLAN["span"] = best[0]
    return sorted(range(n), key=lambda i: (best[1][i], i))


def waits(ops):
    deps = []
    for i, o in enumerate(ops):
        last = {}
        for j in range(i - 1, -1, -1):
            e = ops[j]
            key = e["sem"] or e["q"]
            if key in last or e["quiet"]:
                continue
            if ordered(o, e):
                last[key] = j
        deps.append(sorted(last.values()))
    known = {q: {} for q in "vspgy"}
    clock = {}
    keep = []
    for i, o in enumerate(ops):
        kn = known[o["q"]]
        w = []
        for j in reversed(deps[i]):
            key = ops[j]["sem"] or ops[j]["q"]
            if kn.get(key, -1) >= j:
                continue
            w.append(j)
            kn[key] = j
            for k2, v2 in clock[j].items():
                kn[k2] = max(kn.get(k2, -1), v2)
        keep.append(w)
        clock[i] = dict(kn)
    return keep


def emit(g, T, ops):
    eng = {"v": g.vector, "s": g.scalar, "p": g.tensor, "g": g, "y": g.sync}
    csem = {"v": "cv", "s": "cs", "p": "cp", "g": "cg"}
    if "order" not in PLAN:
        PLAN["order"] = arrange(ops)
        PLAN["keep"] = waits([ops[i] for i in PLAN["order"]])
    ops = [ops[i] for i in PLAN["order"]]
    keep = PLAN["keep"]
    need = set(j for w in keep for j in w)
    count, total, waited = {}, {}, {}
    for i, o in enumerate(ops):
        q = eng[o["q"]]
        for j in keep[i]:
            name, val = count[j]
            q.wait_ge(T.sem[name], val)
            waited[name] = max(waited.get(name, 0), val)
        ins = o["f"](q)
        if o["sem"] is not None:
            total[o["sem"]] = total.get(o["sem"], 0) + 16
            ins.then_inc(T.sem[o["sem"]], 16)
            count[i] = (o["sem"], total[o["sem"]])
        elif i in need:
            name = csem[o["q"]]
            total[name] = total.get(name, 0) + 1
            ins.then_inc(T.sem[name], 1)
            count[i] = (name, total[name])
    for name in total:
        if waited.get(name, 0) < total[name]:
            g.wait_ge(T.sem[name], total[name])


def rank_program(g, core, T, topo):
    rank = T.rank_of(core)
    if rank is None:
        relay_program(g, core, T, topo)
        return
    n = len(T.cores)
    nxt, prv = T.cores[(rank + 1) % n], T.cores[(rank - 1) % n]
    ops = []

    def V(name, lo, hi, step=1):
        return (name, lo, hi, step)

    def P(bank, lo=0, hi=K):
        return ("ps", 512 * bank + lo, 512 * bank + hi, 1)

    def ap(v):
        if not isinstance(v, tuple):
            return v
        return T[v[0]][:, v[1]:v[2]:v[3]] if v[3] > 1 else T[v[0]][:, v[1]:v[2]]

    def tr(v):
        return ("ps", v[1] // 512 * 512, v[1] // 512 * 512 + 512, 1) if v[0] == "ps" else v

    def size(v):
        return len(range(v[1], v[2], v[3]))

    def add(q, f, r, w, d, sem=None, quiet=False, occ=None, after=()):
        ops.append({"q": q, "f": f, "r": [tr(v) for v in r if isinstance(v, tuple)], "w": [tr(v) for v in w], "d": d,
                    "occ": d if occ is None else occ, "sem": sem, "quiet": quiet, "after": list(after)})
        return len(ops) - 1

    def src(v, off):
        return ap(v) if off is None else ap(v).indirect(ap(off))

    def vcost(out, off, per, *sides):
        if off is not None:
            return 0.05 + size(out) * (GAT + (TTG if per == 2.0 else 0.0)) * CYC
        if per is None:
            per = 0.5 if all(WIDE[v[0]] == 2 for v in (out,) + sides) else 1.0
        return VFX + max(64.0, size(out) * per) * CYC + (PSX if any(v[0] == "ps" for v in sides) else 0.0)

    def copy(out, in_, off=None):
        add("v", lambda q: q.tensor_copy(ap(out), src(in_, off)), [in_, off], [out], vcost(out, off, None, in_))

    def tt(out, a, b, op, off=None):
        add("v", lambda q: q.tensor_tensor(ap(out), src(a, off), ap(b), op), [a, b, off], [out],
            vcost(out, off, 1.0 if "ps" in (a[0], b[0]) else 2.0, a, b))

    def ts(out, a, s1, op0, s2=None, op1=None, off=None):
        d = vcost(out, off, None, a)
        if op1 is None:
            add("v", lambda q: q.tensor_scalar(ap(out), src(a, off), ap(s1), None, op0), [a, s1, off], [out], d)
        else:
            add("v", lambda q: q.tensor_scalar(ap(out), src(a, off), ap(s1), ap(s2), op0, op1), [a, s1, s2, off], [out], d)

    def scan(out, d0, d1, init, op0, op1):
        add("v", lambda q: q.tensor_tensor_scan(ap(out), ap(d0), ap(d1), ap(init), op0, op1), [d0, d1, init], [out],
            vcost(out, None, None, d0, d1))

    def least(out, in_):
        add("v", lambda q: q.tensor_reduce(ap(out), ap(in_), AxisListType.X, OP.min), [in_], [out], vcost(in_, None, 1.0))

    def fill(out, c):
        add("v", lambda q: q.memset(ap(out), c), [], [out], vcost(out, None, None))

    def act(out, in_, func, off=None, scale=None, bias=None, acc=None):
        kw = {}
        if scale is not None:
            kw["scale"] = scale
        if bias is not None:
            kw["bias"] = ap(bias)
        if acc is not None:
            kw["accum_out"] = ap(acc)
        d = (0.065 + size(out) * GAT * CYC if off is not None else SFX + size(out) * CYC + (PSX if in_[0] == "ps" else 0.0)) \
            + (0.02 if acc else 0.0)
        add("s", lambda q: q.activation(ap(out), src(in_, off), func, **kw), [in_, off, bias],
            [out] + ([acc] if acc is not None else []), d)

    def quant(c, s, in_):
        add("v", lambda q: q.quantize_mx(ap(c), ap(s), ap(in_)), [in_], [c, s], 0.014 + 0.00023 * size(in_))

    def mm(out, wc, ws, xc, xs, first=(), after=()):
        def f(q):
            for sem, val in first:
                q.wait_ge(T.sem[sem], val)
            return q.matmul_mx(ap(out), ap(wc), ap(ws), ap(xc), ap(xs), True, True)
        return add("p", f, [wc, ws, xc, xs], [out], (size(xc) + 16) * PEC + PFX, after=after)

    def dma(qn, out, in_, r, w, sem, d=2.5, first=(), after=()):
        def f(q):
            for s, val in first:
                q.wait_ge(T.sem[s], val)
            return q.dma_start(out, in_)
        return add(qn, f, r, w, d, sem, occ=0.05, after=after)

    turn = [0]

    def to_list(row, ms=None):
        w = size(row)
        if ms is None:
            ms = ("ms", C * (turn[0] % 4))
            turn[0] += 1
        scan(V(ms[0], ms[1], ms[1] + w), V("cap", 0, w), row, 0.0, OP.add, OP.max)
        return V(ms[0], ms[1] + 15, ms[1] + w, 16)

    OFF, OFFK, NEG1, NEGK1 = V("off", 0, 1), V("off", 1, 2), V("off", 2, 3), V("off", 4, 5)
    BQ, TE, OFFS, POSK, KEY1 = V("off", 6, 7), V("off", 7, 8), V("off", 8, 9), V("off", 9, 10), V("off", 10, 11)
    UR = (V("qr", 0, 128), V("sr", 0, 128))

    def QA(t):
        return V("qx", C * t, C * t + K), V("sx", C * t, C * t + K)

    def QB(t):
        return V("qx", C * t + K, C * t + C), V("sx", C * t + K, C * t + C)

    def planes(lo, hi):
        for b in range(4):
            act(V("xh", C * b + lo, C * b + hi), V("xt", 4 * lo + b, 4 * hi, 4), AF.Copy, scale=0.5)

    def both(out, win, lst, nv):
        if nv:
            copy(V(out[0], out[1], out[1] + 16 * nv), win, V(lst[0], lst[1], lst[1] + nv))
        if lst[1] + nv < lst[2]:
            act(V(out[0], out[1] + 16 * nv, out[2]), win, AF.Copy, off=V(lst[0], lst[1] + nv, lst[2]))

    def odd(name, lo, hi):
        return V(name, 2 * (Z + lo) + 1, 2 * (Z + hi), 2)

    d0 = dma("s", T.ut[:], T.u[:], [], [V("ut", 0, 512)], "du", 4.4)
    d1 = dma("y", T.xt[:, 0:4 * K], T.x[:, 0:4 * K], [], [V("xt", 0, 4 * K)], "dxa", 3.6)
    dma("s", T.ptl[:], T.ptr[:], [], [V("ptl", 0, 28)], "dptr", 4.6, after=[(d0, 0.0)])
    d2 = dma("y", T.xt[:, 4 * K:4 * C], T.x[:, 4 * K:4 * C], [], [V("xt", 4 * K, 4 * C)], "dxb", 5.8, after=[(d1, 0.0)])
    d3 = dma("y", T.qw[:].bitcast(dt.uint8), T.wc[:], [], [V("qw", 0, 512)], "dwc", 7.2, after=[(d2, 0.0)])
    dma("y", T.sw[:], T.ws[:], [], [V("sw", 0, 512)], "dws", 7.8, after=[(d3, 0.0)])
    add("g", lambda q: q.iota(T.pi[:, 0:1], [[0, 1]], 0, 1), [], [V("pi", 0, 1)], 0.14)
    add("g", lambda q: q.iota(T.i16[:, 0:16], [[1, 16]], 0, 0, allow_small_or_imprecise_dtypes=True), [], [V("i16", 0, 16)], 0.16)
    add("g", lambda q: q.iota(T.i16[:, 16:44], [[16, 28]], 0, 0, allow_small_or_imprecise_dtypes=True), [], [V("i16", 16, 44)], 0.19)
    add("g", lambda q: q.iota(T.iom[:], [[1, RW]], -K, 0, allow_small_or_imprecise_dtypes=True), [], [V("iom", 0, RW)], 1.0)
    add("g", lambda q: q.iota(T.iot[:], [[1, RW]], 0, 0, allow_small_or_imprecise_dtypes=True), [], [V("iot", 0, RW)], 1.0)
    fill(V("one", 0, 520), 1.0)
    add("g", lambda q: q.affine_select(T.et[:, 0:516], T.one[:, 0:516], [[-1, 516]], OP.is_equal, 0.0, 3, 4),
        [V("one", 0, 516)], [V("et", 0, 516)], 1.1)
    for nm in ("ra", "rb", "rc", "rd"):
        fill(V(nm, C, RW), float(C - K))
    for nm in ("pw", "pa", "pb"):
        fill(V(nm, 0, 2 * (Z + K)), -float(K + Z))
    for nm in ("ca", "cc"):
        fill(V(nm, 0, 2 * Z), -LIFT)
    fill(V("ca", 2 * Z, 2 * (Z + K)), 1.0)
    for nm in ("da", "db"):
        fill(V(nm, 2 * Z, 2 * (Z + K)), 0.0)
    fill(V("cum", C, RW), -LIFT * (Z - 1))
    fill(POSK, float(K))
    fill(V("kk", 0, K), LIFT)
    fill(V("asc", 0, K), 0.0)
    fill(NEG1, -1.0)
    fill(NEGK1, -float(K + 1))
    ts(V("pq", 0, 1), V("pi", 0, 1), 15, OP.bitwise_and)
    copy(V("qf", 0, 1), V("pq", 0, 1))
    Q = V("qf", 0, 1)
    ts(V("qf", 1, 2), Q, 1.0, OP.add)
    ts(OFF, Q, 14.5, OP.is_lt, LIFT, OP.mult)
    ts(V("qo", 0, 28), V("one", 0, 28), Q, OP.mult)
    ts(OFFK, OFF, float(K), OP.subtract)
    ts(OFFS, OFF, K + Z + 0.5, OP.subtract)
    ts(BQ, Q, -16.0, OP.mult, RBASE + 120.0, OP.add)
    ts(V("qf", 2, 3), Q, NK - 1.0, OP.min, 16.0, OP.mult)
    ts(TE, V("qf", 2, 3), 15.5, OP.add, -LIFT, OP.mult)
    ts(V("qf", 3, 4), Q, NK - 1.5, OP.is_gt, LIFT, OP.mult)
    ts(V("qf", 4, 5), Q, 16.0, OP.mult, 15.0, OP.add)
    tt(KEY1, V("qf", 3, 4), V("qf", 4, 5), OP.add)
    I16 = V("i16", 0, 16)
    ts(V("w16", 0, 16), I16, Q, OP.is_equal, -2 * BIG, OP.mult)
    ts(V("w16", 16, 32), I16, 0.5, OP.is_lt, 2 * BIG, OP.mult)
    ts(V("w16", 32, 48), I16, Q, OP.is_equal, -2 * LIFT, OP.mult)
    ts(V("w16", 48, 64), I16, V("qf", 1, 2), OP.is_equal, LIFT, OP.mult)
    ts(V("w16", 64, 80), I16, 0.5, OP.is_gt)
    ts(V("w16", 0, 16), V("w16", 0, 16), BIG, OP.add)
    ts(V("w16", 16, 32), V("w16", 16, 32), BIG, OP.subtract)
    tt(V("w16", 32, 48), V("w16", 32, 48), V("w16", 48, 64), OP.add)
    ts(V("ce", 0, 16), I16, 256.0, OP.mult, RBASE + 256.0, OP.add)
    act(V("mk", 0, K), V("w16", 0, 16), AF.Copy, off=V("qo", 0, NK))
    act(V("rst", 0, K), V("w16", 16, 32), AF.Copy, off=V("qo", 0, NK))
    act(V("keep", 0, K), V("w16", 64, 80), AF.Copy, off=V("qo", 0, NK))
    act(V("cap", 0, C), V("w16", 32, 48), AF.Copy, off=V("qo", 0, 28))
    quant(V("qu", 0, 128), V("su", 0, 128), V("ut", 0, 512))
    copy(V("uo", 0, 8), V("i16", 16, 24))
    add("v", lambda q: q.tensor_copy(T.qr[:, 0:128].bitcast(dt.uint32), T.qu[:, 0:128].bitcast(dt.uint32).indirect(T.uo[:, 0:8])),
        [V("qu", 0, 128), V("uo", 0, 8)], [V("qr", 0, 128)], 0.22)
    act(V("sr", 0, 128), V("su", 0, 128), AF.Copy, off=V("uo", 0, 8))
    for b in range(4):
        quant(V("qe", 128 * b, 128 * b + 128), V("se", 128 * b, 128 * b + 128), V("et", 3 - b, 515 - b))

    def ranks(h, nv, bank, bank2, first):
        row = ("arow", "brow")[h]
        H = K // 2
        act(V(row, 0, K), P(bank2), AF.Copy)
        c = 16 * nv
        for lo, hi in ((c, K), (0, c)):
            tt(V("md", K * h + lo, K * h + hi), P(bank, lo, hi), V("mk", lo, hi), OP.max)
            scan(V("hold", K * h + lo, K * h + hi), V("rst", lo, hi), V("md", K * h + lo, K * h + hi), BIG, OP.max, OP.min)
        tt(V("eq", K * h, K * h + K), P(bank), V("hold", K * h, K * h + K), OP.is_equal)
        scan(V("es", K * h, K * h + K), V("keep", 0, K), V("eq", K * h, K * h + K), 0.0, OP.mult, OP.subtract)
        f0 = NK * W2 * h
        ts(V("fs", f0 + W2 * nv + K + 1, f0 + W2 * NK, W2), V("es", K * h + c + 15, K * h + K, 16), -1.0, OP.mult, -16.0, OP.add)
        for k in range(NK):
            own, c = V("hold", K * h + 16 * k + 15, K * h + 16 * k + 16), 16 * k + 16
            if k < nv:
                f = NK * K * h + K * k
                ts(V("fv", f, f + c), V(row, 0, c), own, OP.is_ge)
                ts(V("fv", f + c, f + K), V(row, c, K), own, OP.is_gt)
                m = NK * H * h + H * k
                scan(V("sm", m, m + H), V("fv", f, f + H), V("fv", f + H, f + K), V("es", K * h + c - 1, K * h + c), OP.add, OP.add)
            else:
                f = f0 + W2 * k
                act(V("fs", f, f + K), V(row, 0, K), AF.Sign, scale=-1.0, bias=own)
                act(V("fs", f, f + c), V("fs", f, f + c), AF.Sign, bias=NEG1, acc=V("fs", f + K, f + K + 1))
                act(V("fs", f + c, f + K + 2), V("fs", f + c, f + K + 2), AF.Relu, scale=-1.0, acc=V("an", 16 * h + k, 16 * h + k + 1))
        m = NK * H * h
        sv, ss = V("sm", m + H - 1, m + H * nv, H), V("an", 16 * h + nv, 16 * h + NK)
        if h == 0:
            ts(V("ku", 0, nv), sv, -1.0, OP.mult, K - 1.0, OP.add)
            ts(V("ku", nv, NK), ss, -1.0, OP.mult, K + 15.0, OP.add)
            add("v", lambda q: q.tensor_copy(T.asc[:, 0:K].indirect(T.ku[:, 0:NK]), T.arow[:, 0:K]),
                [V("arow", 0, K), V("ku", 0, NK)], [V("asc", 0, K)], 0.05 + K * SCA * CYC)
            act(V("krow", 0, K), V("iot", 0, K), AF.Copy, off=V("ku", 0, NK))
            if first:
                copy(V("kl", 0, NK), V("ku", 0, NK))
            else:
                tt(V("p16", 0, NK), V("asc", 15, K, 16), V("w16", 0, NK), OP.max)
                least(V("sc", 0, 1), V("p16", 0, NK))
        else:
            copy(V("ru", 0, nv), sv)
            ts(V("ru", nv, NK), ss, -16.0, OP.add)
            if first:
                copy(V("kl", NK, 2 * NK), V("ru", 0, NK))

    EU, AU, NB = V("eu", 0, NK), V("au", 0, NK), V("sc", 4, 5)

    def LST(s, lo=0, hi=NK):
        return V("lp", 16 * s + lo, 16 * s + hi)

    def spaced(out, lst):
        ts(out, lst, OFFS, OP.subtract, 2.0, OP.mult)

    def gather2(name, win, s, nv, lo=0):
        mid = max(lo, 16 * nv)
        if mid > lo:
            copy(odd(name, lo, mid), win, LST(s, lo // 16, nv))
        if mid < K:
            act(odd(name, mid, K), win, AF.Copy, off=LST(s, mid // 16, NK))

    def powers(lst, off):
        ts(V("nu", 0, NK), lst, off, OP.subtract, float(C), OP.min)
        act(odd("pw", 0, K), V("cum", 0, RW), AF.Identity, off=V("nu", 0, NK), scale=1.0 / LIFT, bias=NEGK1)
        spaced(LST(0), to_list(odd("pw", 0, K)))
        a, s = "pw", 0
        while 2 ** s < JUMP:
            b = "pa" if s % 2 == 0 else "pb"
            lo = JUMP if 2 ** (s + 1) == JUMP else 0
            gather2(b, V(a, 0, 2 * (Z + K)), s, SQV, lo)
            spaced(LST(s + 1, lo // 16, NK), to_list(odd(b, lo, K)))
            a, s = b, s + 1

    def numbers(off):
        tt(V("er", 0, 16), V("iot", 0, C), V("ce", 0, 16), OP.add, off=V("bu", 0, 1))
        tt(V("ne", 0, 16), V("sr4", 0, C), V("er", 0, 16), OP.subtract, off=V("bu", 0, 1))
        ts(EU, V("ne", 0, NK), -1.0, OP.mult)
        ts(V("ef", 0, NK), V("ne", 0, NK), -1.0, OP.mult, off, OP.add)
        for b in range(4):
            act(V("vh", K * b, K * b + K), V("xh", C * b, C * b + C), AF.Copy, off=EU)

    def way(h):
        scan(V("sr4", K * h, K * h + K), V("one", 0, K), V("rr", K * h, K * h + K), V("sr4", K - 1, K) if h else 0.0, OP.add, OP.max)

    def ancestors(t, off):
        lst = to_list(V("xr", 0, K), ("mx", K))
        tt(V("af", 0, NK), lst, V("ef", 0, NK), OP.min)
        ts(AU, V("af", 0, NK), off, OP.subtract)
        if t < R - 1:
            powers(lst, off)

    def first_round():
        nb, nw = V("cb", K - 1, K), C // 16
        tt(V("fb", 0, K), V("asc", 0, K), V("brow", 0, K), OP.is_lt, off=V("ru", 0, NK))
        scan(V("cb", 0, K), V("one", 0, K), V("fb", 0, K), 0.0, OP.mult, OP.add)
        ts(V("fl", 0, NK), V("kl", 0, NK), nb, OP.is_ge)
        ts(V("fl", NK, 2 * NK), V("kl", NK, 2 * NK), nb, OP.is_lt)
        tt(V("t3", 0, nw), V("fl", 0, nw), V("dl", 0, nw), OP.mult)
        tt(V("t4", 0, nw), V("t3", 0, nw), V("pd", 0, nw), OP.add)
        ts(V("ta", 0, K), V("krow", 0, K), nb, OP.is_lt, -LIFT, OP.mult)
        scan(V("cum", 0, K), V("kk", 0, K), V("ta", 0, K), 0.0, OP.add, OP.add)
        ts(V("cum", K, C), V("cb", 0, K), LIFT, OP.mult, V("cum", K - 1, K), OP.add)
        ts(V("rr", 0, C), V("cum", 0, C), 16.0 / LIFT, OP.mult, BQ, OP.add)
        act(V("junk", 0, C), V("cum", 0, C), AF.Sign, bias=TE, acc=V("ea", 0, 1))
        ts(V("bu", 0, 1), V("ea", 0, 1), -0.5, OP.mult, C / 2.0, OP.add)
        way(0)
        way(1)
        numbers(OFFK)
        both(V("xp", 0, K), V("pr", 0, C), EU, XPV)
        ts(V("pe", 0, NK), to_list(V("xp", 0, K), ("mx", 0)), OFFK, OP.subtract)

        def L(s):
            return V("lu", 32 * (s % 4), 32 * (s % 4) + nw)
        copy(L(0), V("t4", 0, nw))
        rows = ["ra", "rb", "rc", "rd"]
        both(V(rows[0], 0, C), V("iom", 0, RW), L(0), SPLIT[0])
        both(V(rows[1], 0, C), V(rows[0], 0, RW), L(0), SPLIT[1])
        for s in range(1, STEPS + 1):
            a, b = rows[s % 4], rows[(s + 1) % 4]
            both(V(b, 0, C), V(a, 0, RW), L(s - 1), SPLIT[s + 1])
            if s < STEPS:
                ts(L(s), to_list(V(a, 0, C)), OFFK, OP.subtract)
        both(V("exb", 0, K), V(a, 0, RW), V("pe", 0, NK), XBV)
        ts(V("yl", 0, NK), to_list(V("exb", 0, K)), OFFK, OP.subtract)
        both(V("xr", 0, K), V(b, 0, RW), V("yl", 0, NK), XV)
        ancestors(0, OFFK)

    def count_over(piv, bound, i):
        H = K // 2
        ts(V("fp", K * i, K * i + K), P(BK_B) if i == 0 else V("brow", 0, K), piv, OP.is_gt)
        scan(V("cp", H * i, H * i + H), V("fp", K * i, K * i + H), V("fp", K * i + H, K * i + K), 0.0, OP.add, OP.add)
        ts(V("gu", 2 * i, 2 * i + 1), V("cp", H * i + H - 1, H * i + H), bound, OP.is_gt)
        return V("gu", 2 * i, 2 * i + 1)

    def marks(h):
        lo, hi = K * h, K * h + K
        scan(V("cum", lo, hi), V("kk", 0, K), V(("ta", "tb")[h], 0, K), V("cum", K - 1, K) if h else 0.0, OP.add, OP.add)
        if RR2[h]:
            ts(V("rr", lo, hi), V("cum", lo, hi), 16.0 / LIFT, OP.mult, BQ, OP.add)
        else:
            act(V("rr", lo, hi), V("cum", lo, hi), AF.Identity, scale=16.0 / LIFT, bias=BQ)
        act(V("junk", lo, hi), V("cum", lo, hi), AF.Sign, bias=TE, acc=V("ea", h, h + 1))
        way(h)

    def later_round(t):
        act(V("j16", 0, 16), I16, AF.Copy, off=count_over(V("sc", 0, 1), KEY1, 0), acc=V("sc", 1, 2))
        ts(V("sc", 2, 3), V("sc", 1, 2), 16.0, OP.mult, Q, OP.add)
        ts(V("gu", 4, 5), V("sc", 1, 2), 16.0, OP.mult, Q, OP.add)
        tt(V("p16", 16, 32), V("asc", 0, K), V("w16", 0, 16), OP.max, off=V("gu", 4, 5))
        least(V("sc", 3, 4), V("p16", 16, 32))
        act(V("j16", 16, 32), I16, AF.Identity, off=count_over(V("sc", 3, 4), V("sc", 2, 3), 1), bias=V("sc", 1, 2), acc=NB)
        ts(V("ta", 0, K), V("krow", 0, K), NB, OP.is_lt, -LIFT, OP.mult)
        scan(odd("ca", 0, K), V("iom", 0, K), V("ta", 0, K), -LIFT, OP.max, OP.add)
        marks(0)
        ts(V("ea", 2, 3), V("ea", 0, 1), -float(C), OP.add)
        a, b, s = "ca", "cc", 0
        while 2 ** s < JUMP:
            d = ("da", "db")[s % 2]
            gather2(d, V(a, 0, 2 * (Z + K)), s, CLV[s])
            scan(V(b, 2 * Z, 2 * (Z + K)), V(d, 2 * Z, 2 * (Z + K)), V(a, 2 * Z, 2 * (Z + K)), 0.0, OP.mult, OP.max)
            a, b, s = b, a, s + 1
        for lo in range(JUMP, K, JUMP):
            hi = min(lo + JUMP, K)
            tt(odd(a, lo, hi), V(a, 0, 2 * (Z + lo)), odd(a, lo, hi), OP.max, off=LST(s, lo // 16, hi // 16))
        act(V("gw", 0, K), V(a, 0, 2 * (Z + K)), AF.Abs, off=LST(0), bias=POSK)
        act(V("gw", K, C), odd(a, 0, K), AF.Abs, bias=POSK)
        ts(V("tb", 0, K), V("iot", 0, K), NB, OP.is_ge, -LIFT, OP.mult, off=V("ru", 0, NK))
        marks(1)
        ts(V("bu", 0, 1), V("ea", 1, 2), V("ea", 2, 3), OP.add, -0.5, OP.mult)
        numbers(OFF)
        both(V("xr", 0, K), V("gw", 0, C), EU, XV)
        ancestors(t, OFF)

    rl = relays(core, nxt, topo)
    en = topo.engines(core, rl[0])
    landed = sum(len(topo.engines(c, core)) for c in relays(prv, core, topo))

    def send(t, qv, sv):
        w = size(qv)
        h, hf = w // 2, len(en) // 2

        def calls(q):
            trs = []
            for i in range(2):
                rid, pid = topo.addr(rl[i], core)
                trs.append(RemoteDMATransfer(dst_ids=[DstId(rid=rid, pnc=pid)], dma_engine_mask=mask_of(en[i * hf:i * hf + hf]),
                                             remote_sem=T.sem["hop" + t],
                                             src=T[qv[0]][:, qv[1] + i * h:qv[1] + i * h + h].bitcast(dt.uint8),
                                             dst=T["rq" + t][:].bitcast(dt.uint8)))
            q.remote_dma_fused(trs, local_sem=T.sem["out" + t])
            rid, pid = topo.addr(rl[2], core)
            q.remote_dma(T["rs" + t][:], ap(sv), T.sem["hop" + t], T.sem["out" + t], pid, rid, mask_of(en))
        return add("g", calls, [qv, sv], [], 0.5, quiet=True)

    def blend(t):
        for b in range(4):
            tt(V("xt", b, 4 * K, 4), V("xh", C * b, C * b + C), V("vh", K * b, K * b + K), OP.add, off=AU)
        quant(QA(t + 1)[0], QA(t + 1)[1], V("xt", 0, 4 * K))
        return send(str(t), QA(t + 1)[0], QA(t + 1)[1])

    def arrive(t, sent):
        first = [("arr%d" % t, landed)] + ([("arrw", landed)] if t == 0 else [])
        after = [(sent, TRAVEL - 0.5)]
        for b in range(4):
            i = mm(P(b), V("lqw", 128 * b, 128 * b + 128), V("lsw", 128 * b, 128 * b + 128),
                   V("lq%d" % t, 0, K), V("ls%d" % t, 0, K), first if b == 0 else (), after)
            after = [(i, 0.0)]
        for b in range(4):
            if EVAC[b] == "s":
                act(V("ht", b, 4 * K, 4), P(b), AF.Relu, scale=0.03125)
            else:
                ts(V("ht", b, 4 * K, 4), P(b), 0.0, OP.max, 0.03125, OP.mult)
        quant(V("qh", 0, K), V("sh", 0, K), V("ht", 0, 4 * K))
        after = []
        for b in range(4):
            i = mm(P(b), V("qe", 128 * b, 128 * b + 128), V("se", 128 * b, 128 * b + 128), V("qh", 0, K), V("sh", 0, K), (), after)
            after = [(i, 0.0)]
        for b in range(4):
            if EVAC2[b] == "s":
                act(V("xt", 4 * K + b, 4 * C, 4), P(b), AF.Copy)
            else:
                copy(V("xt", 4 * K + b, 4 * C, 4), P(b))
        quant(QB(t + 1)[0], QB(t + 1)[1], V("xt", 4 * K, 4 * C))

    def scores(h, q, nv, first=False):
        banks = (BK_A, BK_A2) if h == 0 else (BK_B, BK_B2)
        for bk in banks:
            mm(P(bk), UR[0], UR[1], q[0], q[1])
        ranks(h, nv, banks[0], banks[1], first)

    copy(V("pf", 0, 28), V("ptl", 0, 28))
    ts(V("il", 0, 28), V("i16", 16, 44), Q, OP.add)
    tt(V("t1", 0, 28), V("pf", 0, 28), V("il", 0, 28), OP.is_equal)
    ts(V("t2", 0, 28), V("t1", 0, 28), float(C), OP.mult)
    tt(V("pd", 0, 28), V("t2", 0, 28), V("pf", 0, 28), OP.max)
    tt(V("dl", 0, 28), V("il", 0, 28), V("pd", 0, 28), OP.subtract)
    copy(V("pu", 0, 28), V("pd", 0, 28))
    act(V("pr", 0, C), V("iom", 0, RW), AF.Copy, off=V("pu", 0, 28))
    quant(QA(0)[0], QA(0)[1], V("xt", 0, 4 * K))
    scores(0, QA(0), NV["a0"], True)
    send("w", V("qw", 0, 512), V("sw", 0, 512))
    quant(QB(0)[0], QB(0)[1], V("xt", 4 * K, 4 * C))
    scores(1, QB(0), NV["b0"], True)
    planes(0, C)
    for t in range(R):
        if t == 0:
            first_round()
        else:
            later_round(t)
        sent = blend(t)
        if t < R - 1:
            scores(0, QA(t + 1), NV["a"])
            planes(0, K)
            arrive(t, sent)
            scores(1, QB(t + 1), NV["b"])
            planes(K, C)
        else:
            qa, qb, s0 = QA(R), QB(R), C * R
            mm(P(BK_A), V("qu", 0, 128), V("su", 0, 128), qa[0], qa[1])
            act(V("prow", 0, K), V("cum", 0, C), AF.Identity, off=AU, scale=1.0 / LIFT, bias=NEG1)
            copy(V("prow", K, C), V("iot", 0, K))
            copy(V("yt", 0, K), P(BK_A))
            i = dma("y", T.oc[:, 0:4 * K], ap(qa[0]).bitcast(dt.uint8), [qa[0]], [], "st", first=[("out%d" % t, 2 * len(en))],
                    after=[(sent, 1.5)])
            i = dma("y", T.pl[:], T.prow[0:128:16, :], [V("prow", 0, C)], [], "st", after=[(i, 0.0)])
            i = dma("y", T.y[:, 0:K], T.yt[:, 0:K], [V("yt", 0, K)], [], "st", after=[(i, 0.0)])
            arrive(t, sent)
            mm(P(BK_B), V("qu", 0, 128), V("su", 0, 128), qb[0], qb[1])
            dma("y", T.oc[:, 4 * K:4 * C], ap(qb[0]).bitcast(dt.uint8), [qb[0]], [], "st", after=[(i, 0.0)])
            for k in range(4):
                dma("y" if k < 2 else "s", T.osc[4 * k:4 * k + 4, :], T.sx[32 * k:32 * k + 4, s0:s0 + C], [V("sx", s0, s0 + C)], [], "st",
                    after=[(i, 0.0)])
            copy(V("yt", K, C), P(BK_B))
            dma("s", T.y[:, K:C], T.yt[:, K:C], [V("yt", K, C)], [], "st", 3.0)
    emit(g, T, ops)
    for t, w in STAGES:
        g.wait_ge(T.sem["out" + t], 2 * len(en))
